import numpy as np
import ml_dtypes


def mxq(x, axis, fmt="e4m3"):
    dtype, down = {"e4m3": (ml_dtypes.float8_e4m3fn, 7), "e5m2": (ml_dtypes.float8_e5m2, 14)}[fmt]
    v = np.moveaxis(np.asarray(x, np.float32).astype(ml_dtypes.bfloat16).astype(np.float64), axis, -1)
    blocks = v.reshape(v.shape[:-1] + (-1, 32))
    amax = np.abs(blocks).max(-1, keepdims=True)
    byte = np.maximum(np.where(amax > 0, np.frexp(amax)[1] - 1 + 127, 0) - down, 1)
    scale = np.exp2(byte - 127.0)
    codes = (blocks / scale).astype(np.float32).astype(dtype).astype(np.float64)
    return np.moveaxis((codes * scale).reshape(v.shape), -1, axis)


WIDE = False


def mx_kscale(k):
    if not WIDE:
        return np.ones(k)
    levels = np.array([10, -10, 5, -5, 0])
    if k % 512:
        return np.exp2(np.random.permutation(np.resize(levels, k // 32))).repeat(32)
    a = np.empty((k // 512, 16))
    for p in range(k // 512):
        a[p, :8] = np.random.permutation(np.resize(levels, 8))
        for g in range(8):
            far = levels[np.abs(levels - a[p, g]) >= 10]
            a[p, g + 8] = far[np.random.randint(len(far))]
    return np.exp2(a.ravel()).repeat(32)


def f64(x):
    return np.asarray(x).astype(np.float64)


def striped(idx):
    return np.tile(idx.reshape(-1, 16).T, (8, 1)).astype(np.uint16)


def unstriped(offs):
    return offs[:16].T.reshape(-1).astype(np.int64)


E2M1 = np.array([0.0, 0.5, 1.0, 1.5, 2.0, 3.0, 4.0, 6.0, -0.0, -0.5, -1.0, -1.5, -2.0, -3.0, -4.0, -6.0])


def pack_weight(w, fmt):
    k, n = w.shape
    w = f64(np.asarray(w, np.float32).astype(ml_dtypes.bfloat16)).reshape(k // 32, 32, n)
    amax = np.abs(w).max(1)
    if fmt == "e4m3":
        byte = np.frexp(amax)[1] - 1 + 127 - 7
    else:
        mant, ex = np.frexp(amax / 6.0)
        byte = np.where(mant > 0.5, ex, ex - 1) + 127
    byte = np.clip(np.where(amax > 0, byte, 1), 1, 254)
    scaled = (w * np.exp2(127.0 - byte)[:, None, :]).reshape(k, n).astype(np.float32)
    by_word = np.ascontiguousarray(scaled.reshape(k // 512, 128, 4, n).transpose(0, 1, 3, 2))
    if fmt == "e4m3":
        words = by_word.astype(ml_dtypes.float8_e4m3fn).view(np.uint8)
    else:
        c = by_word.astype(ml_dtypes.float4_e2m1fn).view(np.uint8) & 0xF
        words = (c[..., 0::2] | (c[..., 1::2] << 4)).reshape(k // 512, 128, 2 * n)
    return np.ascontiguousarray(words), np.ascontiguousarray(byte.astype(np.uint8).reshape(k // 512, 16, n))


def unpack_weight(words, scales, fmt):
    g, _, n = scales.shape
    words = np.ascontiguousarray(words).reshape(g, 128, n, -1)
    if fmt == "e4m3":
        vals = words.view(ml_dtypes.float8_e4m3fn).astype(np.float64)
    else:
        nib = np.empty((g, 128, n, 4), np.uint8)
        nib[..., 0::2] = words & 0xF
        nib[..., 1::2] = words >> 4
        vals = E2M1[nib]
    vals = vals * np.repeat(np.exp2(scales.astype(np.float64) - 127.0), 8, axis=1)[..., None]
    return vals.transpose(0, 1, 3, 2).reshape(g * 512, n)


def d_relu2(v):
    return 2.0 * np.maximum(v, 0.0)


K, T, E, C, H, N = 256, 512, 8, 128, 512, 512


def by_expert(wq, xq):
    return np.concatenate([wq[e].T @ xq[:, e * C:(e + 1) * C] for e in range(E)], axis=1)


def setup_inputs():
    n = np.random.standard_normal
    v = mx_kscale(N)
    u = mx_kscale(H)
    first = np.random.permutation(np.repeat(np.arange(E), T // E))
    second = (first + 1 + np.random.permutation(np.repeat(np.arange(E - 1), -(-T // (E - 1)))[:T])) % E
    while np.bincount(second, minlength=E).max() != T // E:
        load = np.bincount(second, minlength=E); hi, lo = int(load.argmax()), int(load.argmin())
        t = np.flatnonzero((second == hi) & (first != lo))[0]; second[t] = lo
    slot_token = np.empty(E * C, np.int64); pos = np.empty((2, T), np.int64); fill = np.zeros(E, np.int64)
    place = np.stack([np.random.permutation(C) for _ in range(E)])
    for r, deal in enumerate((first, second)):
        for t in np.random.permutation(T):
            e = deal[t]; j = e * C + place[e, fill[e]]; fill[e] += 1; slot_token[j] = t; pos[r, t] = j
    g = np.random.uniform(0.2, 0.8, T)
    dy = pack_weight(n((N, T)) * v[:, None], "e4m3")
    w2t = [pack_weight(m, "e4m3") for m in n((E, N, H)) / np.sqrt(N) / v[None, :, None] * u]
    w1t = pack_weight(n((H, K)) / np.sqrt(H) / u[:, None], "e4m3")
    return {
        "dy_words": dy[0],
        "dy_scales": dy[1],
        "w2t_words": np.stack([m[0] for m in w2t]),
        "w2t_scales": np.stack([m[1] for m in w2t]),
        "w1t_words": w1t[0],
        "w1t_scales": w1t[1],
        "a": (n((H, T))).astype(np.float32),
        "gate": np.stack([np.tile(g, (128, 1)), np.tile(1.0 - g, (128, 1))]).astype(np.float32),
        "offs": striped(slot_token),
        "pos1": striped(pos[0]),
        "pos2": striped(pos[1]),
    }


def reference(dy_words, dy_scales, w2t_words, w2t_scales, w1t_words, w1t_scales, a, gate, offs, pos1, pos2):
    w2t = np.stack([unpack_weight(w2t_words[e], w2t_scales[e], "e4m3") for e in range(E)])
    w1t = unpack_weight(w1t_words, w1t_scales, "e4m3")
    idx = unstriped(offs)
    gq = unpack_weight(dy_words, dy_scales, "e4m3")[:, idx]
    y = by_expert(w2t, gq)
    dh = sum(f64(gate[r, :1]) * y[:, unstriped(p)] for r, p in enumerate((pos1, pos2)))
    return w1t.T @ mxq(dh * d_relu2(f64(a)), 0, "e4m3")

@@ -1,0 +1,280 @@
+from contextlib import ExitStack
+
+import concourse.mybir as mybir
+from concourse.masks import make_identity
+
+K, T, E, C, H, N = 256, 512, 8, 128, 512, 512
+FLOPS = 2 * N * H * E * C + 2 * H * K * T
+
+F32 = mybir.dt.float32
+BF16 = mybir.dt.bfloat16
+I32 = mybir.dt.int32
+U32 = mybir.dt.uint32
+U16 = mybir.dt.uint16
+U8 = mybir.dt.uint8
+FP8X4 = mybir.dt.float8_e4m3fn_x4
+ACT = mybir.ActivationFunctionType
+MULT = mybir.AluOpType.mult
+ADD = mybir.AluOpType.add
+
+P = 128
+SLOTS = E * C
+ROW_TILES = H // P
+EXPERT_GROUPS = [(0, 2), (2, 4), (4, 6), (6, 7), (7, 8)]
+
+
+def tile_moe_sub_relu2_kernel(
+    tc, dy_words, dy_scales, w2t_words, w2t_scales, w1t_words, w1t_scales, a, gate, offs, pos1, pos2, out
+):
+    nc = tc.nc
+    with ExitStack() as ctx:
+        keep = ctx.enter_context(tc.tile_pool(name="keep", bufs=1))
+        psum = ctx.enter_context(tc.psum_pool(name="psum", bufs=4))
+
+        offs_sb = keep.tile([P, SLOTS // 16], U16, name="offs_sb")
+        pos_sb = [keep.tile([P, T // 16], U16, name="pos_sb%d" % r) for r in range(2)]
+        dy_w = keep.tile([P, T], I32, name="dy_w", align_bytes=64)
+        dy_s = keep.tile([P, T], U8, name="dy_s", align_bytes=64)
+        w2_s = keep.tile([P, E, H], U8, name="w2_s", align_bytes=64)
+        w1_s = keep.tile([P, K], U8, name="w1_s", align_bytes=64)
+        w1_w = keep.tile([P, 4 * K], U8, name="w1_w", align_bytes=64)
+        w2_w = [keep.tile([P, E, 1024], U8, name="w2_w%d" % half, align_bytes=64) for half in range(2)]
+        a_sb = [keep.tile([P, ROW_TILES, 256], F32, name="a_sb%d" % half) for half in range(2)]
+        slope = [keep.tile([P, ROW_TILES, 256], F32, name="slope%d" % half) for half in range(2)]
+        gate_rows = keep.tile([P, T], F32, name="gate_rows")
+        gate_cols = keep.tile([P, 4, 2], F32, name="gate_cols")
+        ident = keep.tile([P, P], F32, name="ident")
+        warm = keep.tile([P, 2], F32, name="warm")
+        y = [keep.tile([P, SLOTS], F32, name="y%d" % t) for t in range(ROW_TILES)]
+
+        def load_scale_rows(queue, plane, rows):
+            for q in range(4):
+                queue.dma_start(out=plane(q).bitcast(I32), in_=rows(q).bitcast(I32))
+
+        def load_w2(half, lo, hi):
+            src = w2t_words[lo:hi].rearrange("e s p i d -> p (e s) (i d)")
+            nc.sync.dma_start(
+                out=w2_w[half][:, lo:hi, :].bitcast(I32), in_=src[:, :, 1024 * half : 1024 * (half + 1)].bitcast(I32)
+            )
+
+        def load_a(half, t_lo, t_hi):
+            nc.sync.dma_start(
+                out=a_sb[half][:, t_lo:t_hi, :],
+                in_=a[P * t_lo : P * t_hi, 256 * half : 256 * (half + 1)].rearrange("(t p) n -> p t n", p=P),
+            )
+
+        nc.vector.memset(dy_s[:].bitcast(I32), 0)
+        nc.vector.memset(w2_s[:].rearrange("p e i -> p (e i)").bitcast(I32), 0)
+        nc.vector.memset(w1_s[:].bitcast(I32), 0)
+        nc.vector.memset(warm[:, 0:1], 0.0)
+        nc.gpsimd.memset(gate_rows[:], 0.0)
+        make_identity(nc, ident[:])
+
+        nc.sync.dma_start(offs_sb[:], offs)
+        nc.sync.dma_start(out=dy_w[:], in_=dy_words[0].rearrange("p t d -> p (t d)").bitcast(I32))
+        load_scale_rows(nc.scalar, lambda q: dy_s[32 * q : 32 * q + 4, :], lambda q: dy_scales[0, 4 * q : 4 * q + 4, :])
+        nc.sync.dma_start(pos_sb[0][:], pos1)
+        load_w2(0, 0, E)
+        nc.scalar.activation(warm[:, 1:2], warm[:, 0:1], ACT.Relu)
+        load_scale_rows(
+            nc.scalar,
+            lambda q: w2_s[32 * q : 32 * q + 4, :, :],
+            lambda q: w2t_scales[:, 0, 4 * q : 4 * q + 4, :].rearrange("e b i -> b e i"),
+        )
+        load_a(0, 0, 2)
+        nc.sync.dma_start(pos_sb[1][:], pos2)
+        load_w2(1, 0, 4)
+        load_w2(1, 4, E)
+        load_a(0, 2, 4)
+        nc.sync.dma_start(out=gate_rows[0:2, :], in_=gate[:, 0, :])
+        load_a(1, 0, 4)
+        nc.sync.dma_start(out=w1_w[:].bitcast(I32), in_=w1t_words[0].rearrange("p k d -> p (k d)").bitcast(I32))
+        load_scale_rows(nc.sync, lambda q: w1_s[32 * q : 32 * q + 4, :], lambda q: w1t_scales[0, 4 * q : 4 * q + 4, :])
+
+        slot_w, slot_s = {}, {}
+        for lo, hi in EXPERT_GROUPS:
+            width = C * (hi - lo)
+            entries = offs_sb[:, lo * C // 16 : hi * C // 16]
+            words = keep.tile([P, width], U32, name="slot_w%d" % lo, align_bytes=64)
+            nc.vector.tensor_copy(words[:], dy_w[:].bitcast(U32).indirect(entries))
+            scales = keep.tile([P, width], U8, name="slot_s%d" % lo, align_bytes=64)
+            nc.vector.tensor_copy(scales[:], dy_s[:].indirect(entries))
+            for e in range(lo, hi):
+                cols = slice(C * (e - lo), C * (e - lo + 1))
+                slot_w[e] = words[:, cols]
+                slot_s[e] = scales[:, cols]
+
+        def expert_products(t, lo, hi, engine_copy):
+            bank = psum.tile([P, 512], F32, name="bank", tag="acc")
+            for e in range(lo, hi):
+                weights = w2_w[t // 2][:, e, 512 * (t % 2) : 512 * (t % 2 + 1)]
+                nc.tensor.matmul_mx(
+                    out=bank[:, C * (e - lo) : C * (e - lo + 1)],
+                    lhsT=weights.bitcast(FP8X4),
+                    lhsT_scale=w2_s[:, e, P * t : P * (t + 1)],
+                    rhs=slot_w[e].bitcast(FP8X4),
+                    rhs_scale=slot_s[e],
+                    start=True,
+                    stop=True,
+                )
+            engine_copy(y[t][:, C * lo : C * hi], bank[:, 0 : C * (hi - lo)])
+
+        def make_slope(half, t_lo, t_hi):
+            nc.scalar.activation(slope[half][:, t_lo:t_hi, :], a_sb[half][:, t_lo:t_hi, :], ACT.Relu, scale=2.0)
+
+        expert_products(0, 0, 4, nc.scalar.copy)
+        expert_products(1, 0, 4, nc.scalar.copy)
+        make_slope(0, 0, 2)
+        expert_products(0, 4, 7, nc.scalar.copy)
+        expert_products(0, 7, 8, nc.vector.tensor_copy)
+        expert_products(1, 4, 8, nc.scalar.copy)
+        expert_products(2, 0, 4, nc.scalar.copy)
+        expert_products(2, 4, 8, nc.scalar.copy)
+        make_slope(0, 2, 4)
+        expert_products(3, 0, 4, nc.scalar.copy)
+        expert_products(3, 4, 8, nc.scalar.copy)
+
+        gate_bank = psum.tile([P, 4, P], F32, name="gate_bank", tag="acc")
+        for c in range(4):
+            nc.tensor.transpose(gate_bank[:, c, :], gate_rows[:, P * c : P * (c + 1)], ident[:])
+        nc.scalar.copy(gate_cols[:], gate_bank[:, :, 0:2])
+        make_slope(1, 0, 4)
+
+        turned = {}
+        gated = {}
+        summed = {}
+        da = keep.tile([P, T, 4], BF16, name="da", align_bytes=64)
+        da_w = keep.tile([P, T], U32, name="da_w", align_bytes=64)
+        da_s = keep.tile([P, T], U8, name="da_s", align_bytes=64)
+
+        def fetch_and_turn(r, t, first, count):
+            lo, hi = P * first, P * (first + count)
+            picked = keep.tile([P, hi - lo], F32, name="picked%d%d%d" % (r, t, first))
+            nc.vector.tensor_tensor(
+                picked[:],
+                y[t][:].indirect(pos_sb[r][:, lo // 16 : hi // 16]),
+                slope[lo // 256][:, t, lo % 256 : lo % 256 + hi - lo],
+                MULT,
+            )
+            for c in range(first, first + count):
+                if (r, c) not in turned:
+                    turned[r, c] = psum.tile([P, H], F32, name="turned", tag="turn")
+                nc.tensor.transpose(
+                    turned[r, c][:, P * t : P * (t + 1)], picked[:, P * (c - first) : P * (c - first + 1)], ident[:]
+                )
+
+        def apply_gate(r, c, t_lo, t_hi):
+            if (r, c) not in gated:
+                gated[r, c] = keep.tile([P, 4, P], F32, name="gated%d%d" % (r, c))
+            nc.scalar.activation(
+                gated[r, c][:, :, 32 * t_lo : 32 * t_hi],
+                turned[r, c][:, P * t_lo : P * t_hi].rearrange("p (m j) -> p j m", j=4),
+                ACT.Copy,
+                scale=gate_cols[:, c, r : r + 1],
+            )
+
+        def turn_back(r, c):
+            if r == 0:
+                summed[c] = psum.tile([P, 4, P], F32, name="summed", tag="acc")
+            for j in range(4):
+                nc.tensor.matmul(
+                    summed[c][:, j, :],
+                    gated[r, c][:, j, :],
+                    ident[:],
+                    start=(r == 0 and j == 0),
+                    stop=(r == 1 and j == 3),
+                    is_transpose=True,
+                )
+
+        def round_da(c, engine_copy):
+            engine_copy(da[:, P * c : P * (c + 1), :], summed[c][:].rearrange("p j n -> p n j"))
+
+        def gate_first_in_pairs(c):
+            gated[0, c] = keep.tile([P, 2, P, 2], F32, name="gated0%d" % c)
+            nc.scalar.activation(
+                gated[0, c][:],
+                turned[0, c][:].rearrange("p (m u e) -> p u m e", u=2, e=2),
+                ACT.Copy,
+                scale=gate_cols[:, c, 0:1],
+            )
+
+        def sum_and_round(c):
+            rounded = keep.tile([P, 2, P, 2], BF16, name="rounded%d" % c)
+            pairs = rounded[:].rearrange("p u m e -> p (u m e)").bitcast(F32)
+            bank = psum.tile([P, 2, P], F32, name="pair_bank", tag="acc")
+            for u in range(2):
+                nc.vector.scalar_tensor_tensor(
+                    rounded[:, u, :, :],
+                    turned[1, c][:].rearrange("p (m u e) -> p u m e", u=2, e=2)[:, u, :, :],
+                    gate_cols[:, c, 1:2],
+                    gated[0, c][:, u, :, :],
+                    MULT,
+                    ADD,
+                )
+                nc.tensor.transpose(bank[:, u, :], pairs[:, P * u : P * (u + 1)], ident[:])
+            nc.scalar.copy(
+                da[:, P * c : P * (c + 1), :].rearrange("p n j -> p (n j)").bitcast(F32).rearrange("p (n u) -> p n u", u=2),
+                bank[:].rearrange("p u n -> p n u"),
+            )
+
+        def quantise(first, count):
+            cols = slice(P * first, P * (first + count))
+            nc.vector.quantize_mx(
+                out=da_w[:, cols].bitcast(FP8X4), scales=da_s[:, cols], in_=da[:, cols, :].rearrange("p n j -> p (n j)")
+            )
+
+        def project(first, count):
+            width = P * count
+            cols = slice(P * first, P * (first + count))
+            bank = psum.tile([P, 2, width], F32, name="out_bank", tag="acc")
+            for h in range(2):
+                nc.tensor.matmul_mx(
+                    out=bank[:, h, :],
+                    lhsT=w1_w[:, 512 * h : 512 * (h + 1)].bitcast(FP8X4),
+                    lhsT_scale=w1_s[:, P * h : P * (h + 1)],
+                    rhs=da_w[:, cols].bitcast(FP8X4),
+                    rhs_scale=da_s[:, cols],
+                    start=True,
+                    stop=True,
+                )
+            return bank
+
+        def store(first, count, bank, engine_copy):
+            width = P * count
+            result = keep.tile([P, 2, width], F32, name="result%d" % first)
+            engine_copy(result[:], bank[:])
+            nc.sync.dma_start(
+                out=out[:, P * first : P * (first + count)].rearrange("(h p) n -> p h n", p=P), in_=result[:]
+            )
+
+        for t in range(ROW_TILES):
+            for r in range(2):
+                fetch_and_turn(r, t, 0, 2)
+            if t % 2 == 1:
+                for r in range(2):
+                    for c in range(2):
+                        apply_gate(r, c, t - 1, t + 1)
+        for r in range(2):
+            for t in range(ROW_TILES):
+                fetch_and_turn(r, t, 2, 1)
+            turn_back(0, r)
+            turn_back(1, r)
+            round_da(r, nc.scalar.copy)
+        gate_first_in_pairs(2)
+        for t in range(ROW_TILES):
+            fetch_and_turn(0, t, 3, 1)
+        gate_first_in_pairs(3)
+        for t in range(2):
+            fetch_and_turn(1, t, 3, 1)
+        quantise(0, 2)
+        store(0, 2, project(0, 2), nc.scalar.copy)
+        for t in range(2, ROW_TILES):
+            fetch_and_turn(1, t, 3, 1)
+        sum_and_round(2)
+        sum_and_round(3)
+        quantise(2, 1)
+        second_bank = project(2, 1)
+        quantise(3, 1)
+        third_bank = project(3, 1)
+        store(2, 1, second_bank, nc.scalar.copy)
+        store(3, 1, third_bank, nc.vector.tensor_copy)

@@ -63,28 +63,32 @@ def tile_moe_sub_relu2_kernel(
                 in_=a[P * t_lo : P * t_hi, 256 * half : 256 * (half + 1)].rearrange("(t p) n -> p t n", p=P),
             )
 
-        nc.vector.memset(dy_s[:].bitcast(I32), 0)
-        nc.vector.memset(w2_s[:].rearrange("p e i -> p (e i)").bitcast(I32), 0)
+        nc.vector.memset(w2_s[:, 0:5, :].rearrange("p e i -> p (e i)").bitcast(I32), 0)
+        nc.gpsimd.memset(w2_s[:, 5:E, :].rearrange("p e i -> p (e i)").bitcast(I32), 0)
         nc.vector.memset(w1_s[:].bitcast(I32), 0)
+        nc.vector.memset(gate_rows[:], 0.0)
         nc.vector.memset(warm[:, 0:1], 0.0)
-        nc.gpsimd.memset(gate_rows[:], 0.0)
         make_identity(nc, ident[:])
 
         nc.sync.dma_start(offs_sb[:], offs)
         nc.sync.dma_start(out=dy_w[:], in_=dy_words[0].rearrange("p t d -> p (t d)").bitcast(I32))
-        load_scale_rows(nc.scalar, lambda q: dy_s[32 * q : 32 * q + 4, :], lambda q: dy_scales[0, 4 * q : 4 * q + 4, :])
-        nc.sync.dma_start(pos_sb[0][:], pos1)
-        load_w2(0, 0, E)
-        nc.scalar.activation(warm[:, 1:2], warm[:, 0:1], ACT.Relu)
+        load_scale_rows(
+            nc.scalar,
+            lambda q: dy_s[32 * q : 32 * (q + 1), :],
+            lambda q: dy_scales[:, 4 * q : 4 * q + 4, :].broadcast_to([8, 4, T]),
+        )
+        load_w2(0, 0, 4)
+        load_w2(0, 4, E)
         load_scale_rows(
             nc.scalar,
             lambda q: w2_s[32 * q : 32 * q + 4, :, :],
             lambda q: w2t_scales[:, 0, 4 * q : 4 * q + 4, :].rearrange("e b i -> b e i"),
         )
+        nc.scalar.activation(warm[:, 1:2], warm[:, 0:1], ACT.Relu)
         load_a(0, 0, 2)
+        nc.sync.dma_start(pos_sb[0][:], pos1)
         nc.sync.dma_start(pos_sb[1][:], pos2)
-        load_w2(1, 0, 4)
-        load_w2(1, 4, E)
+        load_w2(1, 0, E)
         load_a(0, 2, 4)
         nc.sync.dma_start(out=gate_rows[0:2, :], in_=gate[:, 0, :])
         load_a(1, 0, 4)

@@ -16,11 +16,15 @@ FP8X4 = mybir.dt.float8_e4m3fn_x4
 ACT = mybir.ActivationFunctionType
 MULT = mybir.AluOpType.mult
 ADD = mybir.AluOpType.add
+MAX = mybir.AluOpType.max
 
 P = 128
 SLOTS = E * C
 ROW_TILES = H // P
-EXPERT_GROUPS = [(0, 2), (2, 4), (4, 6), (6, 7), (7, 8)]
+TURNED_BANK = {(0, 0): 4, (0, 1): 5, (1, 0): 6, (1, 1): 7, (0, 2): 0, (1, 2): 4, (0, 3): 2, (1, 3): 5}
+PAIR_BANK = {0: 3, 1: 1, 2: 7, 3: 3}
+OUT_BANK = {(0, 0): 6, (2, 0): 1, (3, 0): 0, (3, 1): 2}
+EXPERT_GROUPS = [(0, 3), (3, 6), (6, 7), (7, 8)]
 
 
 def tile_moe_sub_relu2_kernel(
@@ -29,7 +33,7 @@ def tile_moe_sub_relu2_kernel(
     nc = tc.nc
     with ExitStack() as ctx:
         keep = ctx.enter_context(tc.tile_pool(name="keep", bufs=1))
-        psum = ctx.enter_context(tc.psum_pool(name="psum", bufs=4))
+        psum = ctx.enter_context(tc.psum_pool(name="psum", bufs=1))
 
         offs_sb = keep.tile([P, SLOTS // 16], U16, name="offs_sb")
         pos_sb = [keep.tile([P, T // 16], U16, name="pos_sb%d" % r) for r in range(2)]
@@ -41,8 +45,8 @@ def tile_moe_sub_relu2_kernel(
         w2_w = [keep.tile([P, E, 1024], U8, name="w2_w%d" % half, align_bytes=64) for half in range(2)]
         a_sb = [keep.tile([P, ROW_TILES, 256], F32, name="a_sb%d" % half) for half in range(2)]
         slope = [keep.tile([P, ROW_TILES, 256], F32, name="slope%d" % half) for half in range(2)]
-        gate_rows = keep.tile([P, T], F32, name="gate_rows")
-        gate_cols = keep.tile([P, 4, 2], F32, name="gate_cols")
+        gate_rows = keep.tile([P, 2, P], F32, name="gate_rows")
+        gate_cols = keep.tile([P, 2, 4], F32, name="gate_cols")
         ident = keep.tile([P, P], F32, name="ident")
         warm = keep.tile([P, 2], F32, name="warm")
         y = [keep.tile([P, SLOTS], F32, name="y%d" % t) for t in range(ROW_TILES)]
@@ -71,45 +75,45 @@ def tile_moe_sub_relu2_kernel(
         make_identity(nc, ident[:])
 
         nc.sync.dma_start(offs_sb[:], offs)
-        nc.sync.dma_start(out=dy_w[:], in_=dy_words[0].rearrange("p t d -> p (t d)").bitcast(I32))
-        load_scale_rows(
-            nc.scalar,
-            lambda q: dy_s[32 * q : 32 * (q + 1), :],
-            lambda q: dy_scales[:, 4 * q : 4 * q + 4, :].broadcast_to([8, 4, T]),
-        )
+        for q in range(4):
+            queue = nc.scalar if q < 2 else nc.sync
+            queue.dma_start(
+                out=dy_s[32 * q : 32 * (q + 1), :].bitcast(I32),
+                in_=dy_scales[:, 4 * q : 4 * q + 4, :].broadcast_to([8, 4, T]).bitcast(I32),
+            )
+        nc.scalar.dma_start(out=dy_w[:], in_=dy_words[0].rearrange("p t d -> p (t d)").bitcast(I32))
+        nc.scalar.activation(warm[:, 1:2], warm[:, 0:1], ACT.Relu)
         load_w2(0, 0, 4)
-        load_w2(0, 4, E)
         load_scale_rows(
-            nc.scalar,
+            nc.sync,
             lambda q: w2_s[32 * q : 32 * q + 4, :, :],
             lambda q: w2t_scales[:, 0, 4 * q : 4 * q + 4, :].rearrange("e b i -> b e i"),
         )
-        nc.scalar.activation(warm[:, 1:2], warm[:, 0:1], ACT.Relu)
-        load_a(0, 0, 2)
+        load_w2(0, 4, E)
+        load_a(0, 0, 4)
         nc.sync.dma_start(pos_sb[0][:], pos1)
         nc.sync.dma_start(pos_sb[1][:], pos2)
         load_w2(1, 0, E)
-        load_a(0, 2, 4)
-        nc.sync.dma_start(out=gate_rows[0:2, :], in_=gate[:, 0, :])
+        nc.gpsimd.dma_start(out=gate_rows[0:4, :, :], in_=gate[:, 0, :].rearrange("r (c p) -> c r p", p=P))
         load_a(1, 0, 4)
-        nc.sync.dma_start(out=w1_w[:].bitcast(I32), in_=w1t_words[0].rearrange("p k d -> p (k d)").bitcast(I32))
-        load_scale_rows(nc.sync, lambda q: w1_s[32 * q : 32 * q + 4, :], lambda q: w1t_scales[0, 4 * q : 4 * q + 4, :])
+        nc.gpsimd.dma_start(out=w1_w[:].bitcast(I32), in_=w1t_words[0].rearrange("p k d -> p (k d)").bitcast(I32))
+        load_scale_rows(nc.gpsimd, lambda q: w1_s[32 * q : 32 * q + 4, :], lambda q: w1t_scales[0, 4 * q : 4 * q + 4, :])
 
         slot_w, slot_s = {}, {}
         for lo, hi in EXPERT_GROUPS:
             width = C * (hi - lo)
             entries = offs_sb[:, lo * C // 16 : hi * C // 16]
-            words = keep.tile([P, width], U32, name="slot_w%d" % lo, align_bytes=64)
-            nc.vector.tensor_copy(words[:], dy_w[:].bitcast(U32).indirect(entries))
             scales = keep.tile([P, width], U8, name="slot_s%d" % lo, align_bytes=64)
             nc.vector.tensor_copy(scales[:], dy_s[:].indirect(entries))
+            words = keep.tile([P, width], U32, name="slot_w%d" % lo, align_bytes=64)
+            nc.vector.tensor_copy(words[:], dy_w[:].bitcast(U32).indirect(entries))
             for e in range(lo, hi):
                 cols = slice(C * (e - lo), C * (e - lo + 1))
                 slot_w[e] = words[:, cols]
                 slot_s[e] = scales[:, cols]
 
-        def expert_products(t, lo, hi, engine_copy):
-            bank = psum.tile([P, 512], F32, name="bank", tag="acc")
+        def expert_products(t, lo, hi, bank_no, engine_copy):
+            bank = psum.tile([P, 512], F32, name="bank", tag="bank%d" % bank_no)
             for e in range(lo, hi):
                 weights = w2_w[t // 2][:, e, 512 * (t % 2) : 512 * (t % 2 + 1)]
                 nc.tensor.matmul_mx(
@@ -123,30 +127,24 @@ def tile_moe_sub_relu2_kernel(
                 )
             engine_copy(y[t][:, C * lo : C * hi], bank[:, 0 : C * (hi - lo)])
 
-        def make_slope(half, t_lo, t_hi):
-            nc.scalar.activation(slope[half][:, t_lo:t_hi, :], a_sb[half][:, t_lo:t_hi, :], ACT.Relu, scale=2.0)
+        expert_products(0, 0, 3, 0, nc.scalar.copy)
+        expert_products(0, 3, 7, 1, nc.scalar.copy)
+        nc.vector.tensor_scalar(slope[0][:], a_sb[0][:], 0.0, 2.0, MAX, MULT)
+        expert_products(0, 7, 8, 2, nc.scalar.copy)
+        expert_products(1, 0, 4, 3, nc.scalar.copy)
+        expert_products(1, 4, 8, 0, nc.scalar.copy)
+        for t in (2, 3):
+            for quad in range(2):
+                expert_products(t, 4 * quad, 4 * quad + 4, 2 * t + quad, nc.scalar.copy)
 
-        expert_products(0, 0, 4, nc.scalar.copy)
-        expert_products(1, 0, 4, nc.scalar.copy)
-        make_slope(0, 0, 2)
-        expert_products(0, 4, 7, nc.scalar.copy)
-        expert_products(0, 7, 8, nc.vector.tensor_copy)
-        expert_products(1, 4, 8, nc.scalar.copy)
-        expert_products(2, 0, 4, nc.scalar.copy)
-        expert_products(2, 4, 8, nc.scalar.copy)
-        make_slope(0, 2, 4)
-        expert_products(3, 0, 4, nc.scalar.copy)
-        expert_products(3, 4, 8, nc.scalar.copy)
-
-        gate_bank = psum.tile([P, 4, P], F32, name="gate_bank", tag="acc")
-        for c in range(4):
-            nc.tensor.transpose(gate_bank[:, c, :], gate_rows[:, P * c : P * (c + 1)], ident[:])
-        nc.scalar.copy(gate_cols[:], gate_bank[:, :, 0:2])
-        make_slope(1, 0, 4)
+        gate_bank = psum.tile([P, 2, P], F32, name="gate_bank", tag="bank1")
+        for r in range(2):
+            nc.tensor.transpose(gate_bank[:, r, :], gate_rows[:, r, :], ident[:])
+        nc.scalar.copy(gate_cols[:], gate_bank[:, :, 0:4])
+        nc.scalar.activation(slope[1][:], a_sb[1][:], ACT.Relu, scale=2.0)
 
         turned = {}
         gated = {}
-        summed = {}
         da = keep.tile([P, T, 4], BF16, name="da", align_bytes=64)
         da_w = keep.tile([P, T], U32, name="da_w", align_bytes=64)
         da_s = keep.tile([P, T], U8, name="da_s", align_bytes=64)
@@ -162,60 +160,24 @@ def tile_moe_sub_relu2_kernel(
             )
             for c in range(first, first + count):
                 if (r, c) not in turned:
-                    turned[r, c] = psum.tile([P, H], F32, name="turned", tag="turn")
+                    turned[r, c] = psum.tile([P, H], F32, name="turned", tag="bank%d" % TURNED_BANK[r, c])
                 nc.tensor.transpose(
                     turned[r, c][:, P * t : P * (t + 1)], picked[:, P * (c - first) : P * (c - first + 1)], ident[:]
                 )
 
-        def apply_gate(r, c, t_lo, t_hi):
-            if (r, c) not in gated:
-                gated[r, c] = keep.tile([P, 4, P], F32, name="gated%d%d" % (r, c))
-            nc.scalar.activation(
-                gated[r, c][:, :, 32 * t_lo : 32 * t_hi],
-                turned[r, c][:, P * t_lo : P * t_hi].rearrange("p (m j) -> p j m", j=4),
-                ACT.Copy,
-                scale=gate_cols[:, c, r : r + 1],
-            )
-
-        def turn_back(r, c):
-            if r == 0:
-                summed[c] = psum.tile([P, 4, P], F32, name="summed", tag="acc")
-            for j in range(4):
-                nc.tensor.matmul(
-                    summed[c][:, j, :],
-                    gated[r, c][:, j, :],
-                    ident[:],
-                    start=(r == 0 and j == 0),
-                    stop=(r == 1 and j == 3),
-                    is_transpose=True,
-                )
-
-        def round_da(c, engine_copy):
-            engine_copy(da[:, P * c : P * (c + 1), :], summed[c][:].rearrange("p j n -> p n j"))
-
-        def gate_first_in_pairs(c):
-            gated[0, c] = keep.tile([P, 2, P, 2], F32, name="gated0%d" % c)
-            nc.scalar.activation(
-                gated[0, c][:],
-                turned[0, c][:].rearrange("p (m u e) -> p u m e", u=2, e=2),
-                ACT.Copy,
-                scale=gate_cols[:, c, 0:1],
-            )
+        def gate_first(c):
+            gated[c] = keep.tile([P, H], F32, name="gated%d" % c)
+            nc.scalar.activation(gated[c][:], turned[0, c][:], ACT.Copy, scale=gate_cols[:, 0, c : c + 1])
 
         def sum_and_round(c):
-            rounded = keep.tile([P, 2, P, 2], BF16, name="rounded%d" % c)
-            pairs = rounded[:].rearrange("p u m e -> p (u m e)").bitcast(F32)
-            bank = psum.tile([P, 2, P], F32, name="pair_bank", tag="acc")
+            rounded = keep.tile([P, H], BF16, name="rounded%d" % c)
+            nc.vector.scalar_tensor_tensor(
+                rounded[:], turned[1, c][:], gate_cols[:, 1, c : c + 1], gated[c][:], MULT, ADD
+            )
+            pairs = rounded[:].bitcast(F32)
+            bank = psum.tile([P, 2, P], F32, name="pair_bank", tag="bank%d" % PAIR_BANK[c])
             for u in range(2):
-                nc.vector.scalar_tensor_tensor(
-                    rounded[:, u, :, :],
-                    turned[1, c][:].rearrange("p (m u e) -> p u m e", u=2, e=2)[:, u, :, :],
-                    gate_cols[:, c, 1:2],
-                    gated[0, c][:, u, :, :],
-                    MULT,
-                    ADD,
-                )
-                nc.tensor.transpose(bank[:, u, :], pairs[:, P * u : P * (u + 1)], ident[:])
+                nc.tensor.transpose(bank[:, u, :], pairs[:, u : 2 * P : 2], ident[:])
             nc.scalar.copy(
                 da[:, P * c : P * (c + 1), :].rearrange("p n j -> p (n j)").bitcast(F32).rearrange("p (n u) -> p n u", u=2),
                 bank[:].rearrange("p u n -> p n u"),
@@ -227,13 +189,12 @@ def tile_moe_sub_relu2_kernel(
                 out=da_w[:, cols].bitcast(FP8X4), scales=da_s[:, cols], in_=da[:, cols, :].rearrange("p n j -> p (n j)")
             )
 
-        def project(first, count):
-            width = P * count
+        def project(first, count, h_lo, h_hi):
             cols = slice(P * first, P * (first + count))
-            bank = psum.tile([P, 2, width], F32, name="out_bank", tag="acc")
-            for h in range(2):
+            bank = psum.tile([P, h_hi - h_lo, P * count], F32, name="out_bank", tag="bank%d" % OUT_BANK[first, h_lo])
+            for h in range(h_lo, h_hi):
                 nc.tensor.matmul_mx(
-                    out=bank[:, h, :],
+                    out=bank[:, h - h_lo, :],
                     lhsT=w1_w[:, 512 * h : 512 * (h + 1)].bitcast(FP8X4),
                     lhsT_scale=w1_s[:, P * h : P * (h + 1)],
                     rhs=da_w[:, cols].bitcast(FP8X4),
@@ -243,42 +204,37 @@ def tile_moe_sub_relu2_kernel(
                 )
             return bank
 
-        def store(first, count, bank, engine_copy):
-            width = P * count
-            result = keep.tile([P, 2, width], F32, name="result%d" % first)
+        def store(first, count, h_lo, h_hi, bank, engine_copy, queue):
+            result = keep.tile([P, h_hi - h_lo, P * count], F32, name="result%d%d" % (first, h_lo))
             engine_copy(result[:], bank[:])
-            nc.sync.dma_start(
-                out=out[:, P * first : P * (first + count)].rearrange("(h p) n -> p h n", p=P), in_=result[:]
+            queue.dma_start(
+                out=out[P * h_lo : P * h_hi, P * first : P * (first + count)].rearrange("(h p) n -> p h n", p=P),
+                in_=result[:],
             )
 
         for t in range(ROW_TILES):
             for r in range(2):
                 fetch_and_turn(r, t, 0, 2)
-            if t % 2 == 1:
-                for r in range(2):
-                    for c in range(2):
-                        apply_gate(r, c, t - 1, t + 1)
-        for r in range(2):
-            for t in range(ROW_TILES):
-                fetch_and_turn(r, t, 2, 1)
-            turn_back(0, r)
-            turn_back(1, r)
-            round_da(r, nc.scalar.copy)
-        gate_first_in_pairs(2)
+        gate_first(0)
+        gate_first(1)
         for t in range(ROW_TILES):
-            fetch_and_turn(0, t, 3, 1)
-        gate_first_in_pairs(3)
-        for t in range(2):
-            fetch_and_turn(1, t, 3, 1)
+            fetch_and_turn(0, t, 2, 2)
+        sum_and_round(0)
+        sum_and_round(1)
+        gate_first(2)
+        gate_first(3)
+        for t in range(ROW_TILES):
+            fetch_and_turn(1, t, 2, 1)
         quantise(0, 2)
-        store(0, 2, project(0, 2), nc.scalar.copy)
-        for t in range(2, ROW_TILES):
+        store(0, 2, 0, 2, project(0, 2, 0, 2), nc.scalar.copy, nc.sync)
+        for t in range(ROW_TILES):
             fetch_and_turn(1, t, 3, 1)
         sum_and_round(2)
         sum_and_round(3)
         quantise(2, 1)
-        second_bank = project(2, 1)
+        third_bank = project(2, 1, 0, 2)
         quantise(3, 1)
-        third_bank = project(3, 1)
-        store(2, 1, second_bank, nc.scalar.copy)
-        store(3, 1, third_bank, nc.vector.tensor_copy)
+        last_banks = [project(3, 1, h, h + 1) for h in range(2)]
+        store(2, 1, 0, 2, third_bank, nc.scalar.copy, nc.sync)
+        store(3, 1, 0, 1, last_banks[0], nc.vector.tensor_copy, nc.sync)
+        store(3, 1, 1, 2, last_banks[1], nc.scalar.copy, nc.scalar)

@@ -39,7 +39,7 @@ def tile_moe_sub_relu2_kernel(
         pos_sb = [keep.tile([P, T // 16], U16, name="pos_sb%d" % r) for r in range(2)]
         dy_w = keep.tile([P, T], I32, name="dy_w", align_bytes=64)
         dy_s = keep.tile([P, T], U8, name="dy_s", align_bytes=64)
-        w2_s = keep.tile([P, E, H], U8, name="w2_s", align_bytes=64)
+        w2_s = keep.tile([P, E // 4, H], U8, name="w2_s", align_bytes=64)
         w1_s = keep.tile([P, K], U8, name="w1_s", align_bytes=64)
         w1_w = keep.tile([P, 4 * K], U8, name="w1_w", align_bytes=64)
         w2_w = [keep.tile([P, E, 1024], U8, name="w2_w%d" % half, align_bytes=64) for half in range(2)]
@@ -55,6 +55,13 @@ def tile_moe_sub_relu2_kernel(
             for q in range(4):
                 queue.dma_start(out=plane(q).bitcast(I32), in_=rows(q).bitcast(I32))
 
+        def load_w2_scales(g):
+            load_scale_rows(
+                nc.sync,
+                lambda q: w2_s[32 * q : 32 * q + 16, g, :],
+                lambda q: w2t_scales[4 * g : 4 * g + 4, 0, 4 * q : 4 * q + 4, :],
+            )
+
         def load_w2(half, lo, hi):
             src = w2t_words[lo:hi].rearrange("e s p i d -> p (e s) (i d)")
             nc.sync.dma_start(
@@ -67,8 +74,7 @@ def tile_moe_sub_relu2_kernel(
                 in_=a[P * t_lo : P * t_hi, 256 * half : 256 * (half + 1)].rearrange("(t p) n -> p t n", p=P),
             )
 
-        nc.vector.memset(w2_s[:, 0:5, :].rearrange("p e i -> p (e i)").bitcast(I32), 0)
-        nc.gpsimd.memset(w2_s[:, 5:E, :].rearrange("p e i -> p (e i)").bitcast(I32), 0)
+        nc.vector.memset(w2_s[:].rearrange("p g i -> p (g i)").bitcast(I32), 0)
         nc.vector.memset(w1_s[:].bitcast(I32), 0)
         nc.vector.memset(gate_rows[:], 0.0)
         nc.vector.memset(warm[:, 0:1], 0.0)
@@ -84,20 +90,17 @@ def tile_moe_sub_relu2_kernel(
         nc.scalar.dma_start(out=dy_w[:], in_=dy_words[0].rearrange("p t d -> p (t d)").bitcast(I32))
         nc.scalar.activation(warm[:, 1:2], warm[:, 0:1], ACT.Relu)
         load_w2(0, 0, 4)
-        load_scale_rows(
-            nc.sync,
-            lambda q: w2_s[32 * q : 32 * q + 4, :, :],
-            lambda q: w2t_scales[:, 0, 4 * q : 4 * q + 4, :].rearrange("e b i -> b e i"),
-        )
+        load_w2_scales(0)
         load_w2(0, 4, E)
-        load_a(0, 0, 4)
+        load_w2_scales(1)
         nc.sync.dma_start(pos_sb[0][:], pos1)
         nc.sync.dma_start(pos_sb[1][:], pos2)
+        load_a(0, 0, 4)
         load_w2(1, 0, E)
         nc.gpsimd.dma_start(out=gate_rows[0:4, :, :], in_=gate[:, 0, :].rearrange("r (c p) -> c r p", p=P))
         load_a(1, 0, 4)
-        nc.gpsimd.dma_start(out=w1_w[:].bitcast(I32), in_=w1t_words[0].rearrange("p k d -> p (k d)").bitcast(I32))
-        load_scale_rows(nc.gpsimd, lambda q: w1_s[32 * q : 32 * q + 4, :], lambda q: w1t_scales[0, 4 * q : 4 * q + 4, :])
+        nc.sync.dma_start(out=w1_w[:].bitcast(I32), in_=w1t_words[0].rearrange("p k d -> p (k d)").bitcast(I32))
+        load_scale_rows(nc.sync, lambda r: w1_s[r:P:32, :], lambda r: w1t_scales[0, r:16:4, :])
 
         slot_w, slot_s = {}, {}
         for lo, hi in EXPERT_GROUPS:
@@ -119,7 +122,7 @@ def tile_moe_sub_relu2_kernel(
                 nc.tensor.matmul_mx(
                     out=bank[:, C * (e - lo) : C * (e - lo + 1)],
                     lhsT=weights.bitcast(FP8X4),
-                    lhsT_scale=w2_s[:, e, P * t : P * (t + 1)],
+                    lhsT_scale=w2_s[4 * (e % 4) : P, e // 4, P * t : P * (t + 1)],
                     rhs=slot_w[e].bitcast(FP8X4),
                     rhs_scale=slot_s[e],
                     start=True,

@@ -24,6 +24,7 @@ ROW_TILES = H // P
 TURNED_BANK = {(0, 0): 4, (0, 1): 5, (1, 0): 6, (1, 1): 7, (0, 2): 0, (1, 2): 4, (0, 3): 2, (1, 3): 5}
 PAIR_BANK = {0: 3, 1: 1, 2: 7, 3: 3}
 OUT_BANK = {(0, 0): 6, (2, 0): 1, (3, 0): 0, (3, 1): 2}
+A_PIECES = [(0, 0, 2), (0, 2, 4), (1, 0, 4)]
 EXPERT_GROUPS = [(0, 3), (3, 6), (6, 7), (7, 8)]
 
 
@@ -43,12 +44,14 @@ def tile_moe_sub_relu2_kernel(
         w1_s = keep.tile([P, K], U8, name="w1_s", align_bytes=64)
         w1_w = keep.tile([P, 4 * K], U8, name="w1_w", align_bytes=64)
         w2_w = [keep.tile([P, E, 1024], U8, name="w2_w%d" % half, align_bytes=64) for half in range(2)]
-        a_sb = [keep.tile([P, ROW_TILES, 256], F32, name="a_sb%d" % half) for half in range(2)]
-        slope = [keep.tile([P, ROW_TILES, 256], F32, name="slope%d" % half) for half in range(2)]
-        gate_rows = keep.tile([P, 2, P], F32, name="gate_rows")
+        a_sb = {}
+        slope = {}
+        for half, t_lo, t_hi in A_PIECES:
+            a_sb[half, t_lo] = keep.tile([P, t_hi - t_lo, 256], F32, name="a_sb%d%d" % (half, t_lo))
+            slope[half, t_lo] = keep.tile([P, t_hi - t_lo, 256], F32, name="slope%d%d" % (half, t_lo))
+        gate_rows = keep.tile([P, P], F32, name="gate_rows")
         gate_cols = keep.tile([P, 2, 4], F32, name="gate_cols")
         ident = keep.tile([P, P], F32, name="ident")
-        warm = keep.tile([P, 2], F32, name="warm")
         y = [keep.tile([P, SLOTS], F32, name="y%d" % t) for t in range(ROW_TILES)]
 
         def load_scale_rows(queue, plane, rows):
@@ -70,14 +73,13 @@ def tile_moe_sub_relu2_kernel(
 
         def load_a(half, t_lo, t_hi):
             nc.sync.dma_start(
-                out=a_sb[half][:, t_lo:t_hi, :],
+                out=a_sb[half, t_lo][:],
                 in_=a[P * t_lo : P * t_hi, 256 * half : 256 * (half + 1)].rearrange("(t p) n -> p t n", p=P),
             )
 
         nc.vector.memset(w2_s[:].rearrange("p g i -> p (g i)").bitcast(I32), 0)
         nc.vector.memset(w1_s[:].bitcast(I32), 0)
         nc.vector.memset(gate_rows[:], 0.0)
-        nc.vector.memset(warm[:, 0:1], 0.0)
         make_identity(nc, ident[:])
 
         nc.sync.dma_start(offs_sb[:], offs)
@@ -88,16 +90,16 @@ def tile_moe_sub_relu2_kernel(
                 in_=dy_scales[:, 4 * q : 4 * q + 4, :].broadcast_to([8, 4, T]).bitcast(I32),
             )
         nc.scalar.dma_start(out=dy_w[:], in_=dy_words[0].rearrange("p t d -> p (t d)").bitcast(I32))
-        nc.scalar.activation(warm[:, 1:2], warm[:, 0:1], ACT.Relu)
         load_w2(0, 0, 4)
         load_w2_scales(0)
         load_w2(0, 4, E)
         load_w2_scales(1)
         nc.sync.dma_start(pos_sb[0][:], pos1)
         nc.sync.dma_start(pos_sb[1][:], pos2)
-        load_a(0, 0, 4)
+        load_a(0, 0, 2)
         load_w2(1, 0, E)
-        nc.gpsimd.dma_start(out=gate_rows[0:4, :, :], in_=gate[:, 0, :].rearrange("r (c p) -> c r p", p=P))
+        load_a(0, 2, 4)
+        nc.gpsimd.dma_start(out=gate_rows[0:8, :], in_=gate[:, 0, :].rearrange("r (c p) -> r c p", p=P))
         load_a(1, 0, 4)
         nc.sync.dma_start(out=w1_w[:].bitcast(I32), in_=w1t_words[0].rearrange("p k d -> p (k d)").bitcast(I32))
         load_scale_rows(nc.sync, lambda r: w1_s[r:P:32, :], lambda r: w1t_scales[0, r:16:4, :])
@@ -132,7 +134,7 @@ def tile_moe_sub_relu2_kernel(
 
         expert_products(0, 0, 3, 0, nc.scalar.copy)
         expert_products(0, 3, 7, 1, nc.scalar.copy)
-        nc.vector.tensor_scalar(slope[0][:], a_sb[0][:], 0.0, 2.0, MAX, MULT)
+        nc.vector.tensor_scalar(slope[0, 0][:], a_sb[0, 0][:], 0.0, 2.0, MAX, MULT)
         expert_products(0, 7, 8, 2, nc.scalar.copy)
         expert_products(1, 0, 4, 3, nc.scalar.copy)
         expert_products(1, 4, 8, 0, nc.scalar.copy)
@@ -140,11 +142,10 @@ def tile_moe_sub_relu2_kernel(
             for quad in range(2):
                 expert_products(t, 4 * quad, 4 * quad + 4, 2 * t + quad, nc.scalar.copy)
 
-        gate_bank = psum.tile([P, 2, P], F32, name="gate_bank", tag="bank1")
-        for r in range(2):
-            nc.tensor.transpose(gate_bank[:, r, :], gate_rows[:, r, :], ident[:])
-        nc.scalar.copy(gate_cols[:], gate_bank[:, :, 0:4])
-        nc.scalar.activation(slope[1][:], a_sb[1][:], ACT.Relu, scale=2.0)
+        gate_bank = psum.tile([P, P], F32, name="gate_bank", tag="bank1")
+        nc.tensor.transpose(gate_bank[:], gate_rows[:], ident[:])
+        nc.scalar.copy(gate_cols[:], gate_bank[:, 0:8].rearrange("p (r c) -> p r c", r=2))
+        nc.scalar.activation(slope[1, 0][:], a_sb[1, 0][:], ACT.Relu, scale=2.0)
 
         turned = {}
         gated = {}
@@ -154,18 +155,23 @@ def tile_moe_sub_relu2_kernel(
 
         def fetch_and_turn(r, t, first, count):
             lo, hi = P * first, P * (first + count)
+            t_lo = 2 * (t // 2) if first < 2 else 0
             picked = keep.tile([P, hi - lo], F32, name="picked%d%d%d" % (r, t, first))
             nc.vector.tensor_tensor(
                 picked[:],
                 y[t][:].indirect(pos_sb[r][:, lo // 16 : hi // 16]),
-                slope[lo // 256][:, t, lo % 256 : lo % 256 + hi - lo],
+                slope[first // 2, t_lo][:, t - t_lo, lo % 256 : lo % 256 + hi - lo],
                 MULT,
             )
             for c in range(first, first + count):
                 if (r, c) not in turned:
                     turned[r, c] = psum.tile([P, H], F32, name="turned", tag="bank%d" % TURNED_BANK[r, c])
+                if c < 2:
+                    place = turned[r, c][:, P * t : P * (t + 1)]
+                else:
+                    place = turned[r, c][:].rearrange("n (u p e) -> n p u e", u=2, e=2)[:, 32 * t : 32 * (t + 1)]
                 nc.tensor.transpose(
-                    turned[r, c][:, P * t : P * (t + 1)], picked[:, P * (c - first) : P * (c - first + 1)], ident[:]
+                    place, picked[:, P * (c - first) : P * (c - first + 1)], ident[:]
                 )
 
         def gate_first(c):
@@ -180,11 +186,32 @@ def tile_moe_sub_relu2_kernel(
             pairs = rounded[:].bitcast(F32)
             bank = psum.tile([P, 2, P], F32, name="pair_bank", tag="bank%d" % PAIR_BANK[c])
             for u in range(2):
-                nc.tensor.transpose(bank[:, u, :], pairs[:, u : 2 * P : 2], ident[:])
+                nc.tensor.transpose(bank[:, u, :], pairs[:, P * u : P * (u + 1)], ident[:])
             nc.scalar.copy(
                 da[:, P * c : P * (c + 1), :].rearrange("p n j -> p (n j)").bitcast(F32).rearrange("p (n u) -> p n u", u=2),
                 bank[:].rearrange("p u n -> p n u"),
             )
+
+        def sum_in_bank(c):
+            back = psum.tile([P, 4, P], F32, name="back", tag="bank%d" % PAIR_BANK[c])
+            for r in range(2):
+                both = keep.tile([P, 4, P], F32, name="both%d%d" % (r, c))
+                nc.scalar.activation(
+                    both[:], turned[r, c][:].rearrange("n (p d) -> n d p", d=4), ACT.Copy, scale=gate_cols[:, r, c : c + 1]
+                )
+                for d in range(4):
+                    nc.tensor.matmul(
+                        back[:, d, :],
+                        lhsT=both[:, d, :],
+                        rhs=ident[:],
+                        is_transpose=True,
+                        start=(r == 0 and d == 0),
+                        stop=(r == 1 and d == 3),
+                    )
+            return back
+
+        def round_out(c, back):
+            nc.scalar.copy(da[:, P * c : P * (c + 1), :], back[:].rearrange("p d n -> p n d"))
 
         def quantise(first, count):
             cols = slice(P * first, P * (first + count))
@@ -216,15 +243,16 @@ def tile_moe_sub_relu2_kernel(
             )
 
         for t in range(ROW_TILES):
+            if t == 2:
+                nc.vector.tensor_scalar(slope[0, 2][:], a_sb[0, 2][:], 0.0, 2.0, MAX, MULT)
             for r in range(2):
                 fetch_and_turn(r, t, 0, 2)
-        gate_first(0)
-        gate_first(1)
+        backs = [sum_in_bank(c) for c in range(2)]
         for t in range(ROW_TILES):
             fetch_and_turn(0, t, 2, 2)
-        sum_and_round(0)
-        sum_and_round(1)
+        round_out(0, backs[0])
         gate_first(2)
+        round_out(1, backs[1])
         gate_first(3)
         for t in range(ROW_TILES):
             fetch_and_turn(1, t, 2, 1)

@@ -21,11 +21,21 @@ MAX = mybir.AluOpType.max
 P = 128
 SLOTS = E * C
 ROW_TILES = H // P
-TURNED_BANK = {(0, 0): 4, (0, 1): 5, (1, 0): 6, (1, 1): 7, (0, 2): 0, (1, 2): 4, (0, 3): 2, (1, 3): 5}
-PAIR_BANK = {0: 3, 1: 1, 2: 7, 3: 3}
-OUT_BANK = {(0, 0): 6, (2, 0): 1, (3, 0): 0, (3, 1): 2}
-A_PIECES = [(0, 0, 2), (0, 2, 4), (1, 0, 4)]
+CHUNKS = T // P
+LIST_COLUMN = 16
+QUADRANT = 32
+PLANES = 4
+BANK_SUMMED = 2
+
 EXPERT_GROUPS = [(0, 3), (3, 6), (6, 7), (7, 8)]
+
+A_PIECES = [(0, 1, 0, 512), (1, 2, 0, 256), (2, 4, 0, 256), (1, 4, 256, 512)]
+
+ROW_TILE_3_BANKS = (6, 7, 0, 2)
+GATE_BANK = 1
+TURNED_BANK = {(0, 0): 4, (0, 1): 5, (1, 0): 6, (1, 1): 7, (0, 2): 0, (0, 3): 2, (1, 2): 4, (1, 3): 5}
+RETURN_BANK = {0: 3, 1: 1, 2: 7, 3: 3}
+OUT_BANK = {(0, 0): 6, (2, 0): 1, (3, 0): 0, (3, 1): 2}
 
 
 def tile_moe_sub_relu2_kernel(
@@ -36,46 +46,46 @@ def tile_moe_sub_relu2_kernel(
         keep = ctx.enter_context(tc.tile_pool(name="keep", bufs=1))
         psum = ctx.enter_context(tc.psum_pool(name="psum", bufs=1))
 
-        offs_sb = keep.tile([P, SLOTS // 16], U16, name="offs_sb")
-        pos_sb = [keep.tile([P, T // 16], U16, name="pos_sb%d" % r) for r in range(2)]
+        offs_sb = keep.tile([P, SLOTS // LIST_COLUMN], U16, name="offs_sb")
+        pos_sb = [keep.tile([P, T // LIST_COLUMN], U16, name="pos_sb%d" % r) for r in range(2)]
         dy_w = keep.tile([P, T], I32, name="dy_w", align_bytes=64)
         dy_s = keep.tile([P, T], U8, name="dy_s", align_bytes=64)
-        w2_s = keep.tile([P, E // 4, H], U8, name="w2_s", align_bytes=64)
+        w2_s = keep.tile([P, E // PLANES, H], U8, name="w2_s", align_bytes=64)
         w1_s = keep.tile([P, K], U8, name="w1_s", align_bytes=64)
         w1_w = keep.tile([P, 4 * K], U8, name="w1_w", align_bytes=64)
-        w2_w = [keep.tile([P, E, 1024], U8, name="w2_w%d" % half, align_bytes=64) for half in range(2)]
-        a_sb = {}
-        slope = {}
-        for half, t_lo, t_hi in A_PIECES:
-            a_sb[half, t_lo] = keep.tile([P, t_hi - t_lo, 256], F32, name="a_sb%d%d" % (half, t_lo))
-            slope[half, t_lo] = keep.tile([P, t_hi - t_lo, 256], F32, name="slope%d%d" % (half, t_lo))
+        w2_w = [keep.tile([P, E, 4 * 2 * P], U8, name="w2_w%d" % half, align_bytes=64) for half in range(2)]
+        a_sb = []
+        slope = []
+        slope_of = {}
+        for piece, (t_lo, t_hi, lo, hi) in enumerate(A_PIECES):
+            a_sb.append(keep.tile([P, t_hi - t_lo, hi - lo], F32, name="a_sb%d" % piece))
+            slope.append(keep.tile([P, t_hi - t_lo, hi - lo], F32, name="slope%d" % piece))
+            for t in range(t_lo, t_hi):
+                for chunk in range(lo // P, hi // P):
+                    slope_of[t, chunk] = (piece, t - t_lo, P * chunk - lo)
         gate_rows = keep.tile([P, P], F32, name="gate_rows")
-        gate_cols = keep.tile([P, 2, 4], F32, name="gate_cols")
+        gate_cols = keep.tile([P, 2, CHUNKS], F32, name="gate_cols")
         ident = keep.tile([P, P], F32, name="ident")
         y = [keep.tile([P, SLOTS], F32, name="y%d" % t) for t in range(ROW_TILES)]
 
-        def load_scale_rows(queue, plane, rows):
+        def load_w2_scales(group):
             for q in range(4):
-                queue.dma_start(out=plane(q).bitcast(I32), in_=rows(q).bitcast(I32))
+                nc.sync.dma_start(
+                    out=w2_s[QUADRANT * q : QUADRANT * q + 4 * PLANES, group, :].bitcast(I32),
+                    in_=w2t_scales[PLANES * group : PLANES * (group + 1), 0, 4 * q : 4 * q + 4, :].bitcast(I32),
+                )
 
-        def load_w2_scales(g):
-            load_scale_rows(
-                nc.sync,
-                lambda q: w2_s[32 * q : 32 * q + 16, g, :],
-                lambda q: w2t_scales[4 * g : 4 * g + 4, 0, 4 * q : 4 * q + 4, :],
-            )
-
-        def load_w2(half, lo, hi):
-            src = w2t_words[lo:hi].rearrange("e s p i d -> p (e s) (i d)")
+        def load_w2(half, e_lo, e_hi):
+            src = w2t_words[e_lo:e_hi].rearrange("e s p i d -> p (e s) (i d)")
+            width = 4 * 2 * P
             nc.sync.dma_start(
-                out=w2_w[half][:, lo:hi, :].bitcast(I32), in_=src[:, :, 1024 * half : 1024 * (half + 1)].bitcast(I32)
+                out=w2_w[half][:, e_lo:e_hi, :].bitcast(I32),
+                in_=src[:, :, width * half : width * (half + 1)].bitcast(I32),
             )
 
-        def load_a(half, t_lo, t_hi):
-            nc.sync.dma_start(
-                out=a_sb[half, t_lo][:],
-                in_=a[P * t_lo : P * t_hi, 256 * half : 256 * (half + 1)].rearrange("(t p) n -> p t n", p=P),
-            )
+        def load_a(piece):
+            t_lo, t_hi, lo, hi = A_PIECES[piece]
+            nc.sync.dma_start(out=a_sb[piece][:], in_=a[P * t_lo : P * t_hi, lo:hi].rearrange("(t p) n -> p t n", p=P))
 
         nc.vector.memset(w2_s[:].rearrange("p g i -> p (g i)").bitcast(I32), 0)
         nc.vector.memset(w1_s[:].bitcast(I32), 0)
@@ -86,137 +96,152 @@ def tile_moe_sub_relu2_kernel(
         for q in range(4):
             queue = nc.scalar if q < 2 else nc.sync
             queue.dma_start(
-                out=dy_s[32 * q : 32 * (q + 1), :].bitcast(I32),
-                in_=dy_scales[:, 4 * q : 4 * q + 4, :].broadcast_to([8, 4, T]).bitcast(I32),
+                out=dy_s[QUADRANT * q : QUADRANT * (q + 1), :].bitcast(I32),
+                in_=dy_scales[:, 4 * q : 4 * q + 4, :].broadcast_to([QUADRANT // 4, 4, T]).bitcast(I32),
             )
         nc.scalar.dma_start(out=dy_w[:], in_=dy_words[0].rearrange("p t d -> p (t d)").bitcast(I32))
-        load_w2(0, 0, 4)
-        load_w2_scales(0)
-        load_w2(0, 4, E)
-        load_w2_scales(1)
+        for group in range(E // PLANES):
+            load_w2(0, PLANES * group, PLANES * (group + 1))
+            load_w2_scales(group)
         nc.sync.dma_start(pos_sb[0][:], pos1)
         nc.sync.dma_start(pos_sb[1][:], pos2)
-        load_a(0, 0, 2)
+        load_a(0)
+        load_a(1)
         load_w2(1, 0, E)
-        load_a(0, 2, 4)
-        nc.gpsimd.dma_start(out=gate_rows[0:8, :], in_=gate[:, 0, :].rearrange("r (c p) -> r c p", p=P))
-        load_a(1, 0, 4)
+        load_a(2)
+        nc.gpsimd.dma_start(out=gate_rows[0 : 2 * CHUNKS, :], in_=gate[:, 0, :].rearrange("r (c p) -> r c p", p=P))
+        load_a(3)
         nc.sync.dma_start(out=w1_w[:].bitcast(I32), in_=w1t_words[0].rearrange("p k d -> p (k d)").bitcast(I32))
-        load_scale_rows(nc.sync, lambda r: w1_s[r:P:32, :], lambda r: w1t_scales[0, r:16:4, :])
+        for m in range(4):
+            nc.sync.dma_start(out=w1_s[m:P:QUADRANT, :].bitcast(I32), in_=w1t_scales[0, m:16:4, :].bitcast(I32))
 
         slot_w, slot_s = {}, {}
-        for lo, hi in EXPERT_GROUPS:
-            width = C * (hi - lo)
-            entries = offs_sb[:, lo * C // 16 : hi * C // 16]
-            scales = keep.tile([P, width], U8, name="slot_s%d" % lo, align_bytes=64)
+        for e_lo, e_hi in EXPERT_GROUPS:
+            width = C * (e_hi - e_lo)
+            entries = offs_sb[:, e_lo * C // LIST_COLUMN : e_hi * C // LIST_COLUMN]
+            scales = keep.tile([P, width], U8, name="slot_s%d" % e_lo, align_bytes=64)
             nc.vector.tensor_copy(scales[:], dy_s[:].indirect(entries))
-            words = keep.tile([P, width], U32, name="slot_w%d" % lo, align_bytes=64)
+            words = keep.tile([P, width], U32, name="slot_w%d" % e_lo, align_bytes=64)
             nc.vector.tensor_copy(words[:], dy_w[:].bitcast(U32).indirect(entries))
-            for e in range(lo, hi):
-                cols = slice(C * (e - lo), C * (e - lo + 1))
+            for e in range(e_lo, e_hi):
+                cols = slice(C * (e - e_lo), C * (e - e_lo + 1))
                 slot_w[e] = words[:, cols]
                 slot_s[e] = scales[:, cols]
 
-        def expert_products(t, lo, hi, bank_no, engine_copy):
-            bank = psum.tile([P, 512], F32, name="bank", tag="bank%d" % bank_no)
-            for e in range(lo, hi):
-                weights = w2_w[t // 2][:, e, 512 * (t % 2) : 512 * (t % 2 + 1)]
+        def expert_products(t, e_lo, e_hi, bank_no):
+            bank = psum.tile([P, 4 * C], F32, name="bank", tag="bank%d" % bank_no)
+            for e in range(e_lo, e_hi):
+                weights = w2_w[t // 2][:, e, 4 * P * (t % 2) : 4 * P * (t % 2 + 1)]
                 nc.tensor.matmul_mx(
-                    out=bank[:, C * (e - lo) : C * (e - lo + 1)],
+                    out=bank[:, C * (e - e_lo) : C * (e - e_lo + 1)],
                     lhsT=weights.bitcast(FP8X4),
-                    lhsT_scale=w2_s[4 * (e % 4) : P, e // 4, P * t : P * (t + 1)],
+                    lhsT_scale=w2_s[4 * (e % PLANES) : P, e // PLANES, P * t : P * (t + 1)],
                     rhs=slot_w[e].bitcast(FP8X4),
                     rhs_scale=slot_s[e],
                     start=True,
                     stop=True,
                 )
-            engine_copy(y[t][:, C * lo : C * hi], bank[:, 0 : C * (hi - lo)])
+            nc.scalar.copy(y[t][:, C * e_lo : C * e_hi], bank[:, 0 : C * (e_hi - e_lo)])
 
-        expert_products(0, 0, 3, 0, nc.scalar.copy)
-        expert_products(0, 3, 7, 1, nc.scalar.copy)
-        nc.vector.tensor_scalar(slope[0, 0][:], a_sb[0, 0][:], 0.0, 2.0, MAX, MULT)
-        expert_products(0, 7, 8, 2, nc.scalar.copy)
-        expert_products(1, 0, 4, 3, nc.scalar.copy)
-        expert_products(1, 4, 8, 0, nc.scalar.copy)
-        for t in (2, 3):
-            for quad in range(2):
-                expert_products(t, 4 * quad, 4 * quad + 4, 2 * t + quad, nc.scalar.copy)
+        expert_products(0, 0, 3, 0)
+        expert_products(0, 3, 7, 1)
+        for piece in range(2):
+            nc.vector.tensor_scalar(slope[piece][:], a_sb[piece][:], 0.0, 2.0, MAX, MULT)
+        expert_products(0, 7, 8, 2)
+        expert_products(1, 0, 4, 3)
+        expert_products(1, 4, 8, 0)
+        expert_products(2, 0, 4, 4)
+        expert_products(2, 4, 8, 5)
+        nc.scalar.activation(slope[2][:], a_sb[2][:], ACT.Relu, scale=2.0)
+        for pair, bank_no in enumerate(ROW_TILE_3_BANKS):
+            expert_products(3, 2 * pair, 2 * pair + 2, bank_no)
 
-        gate_bank = psum.tile([P, P], F32, name="gate_bank", tag="bank1")
+        gate_bank = psum.tile([P, P], F32, name="gate_bank", tag="bank%d" % GATE_BANK)
         nc.tensor.transpose(gate_bank[:], gate_rows[:], ident[:])
-        nc.scalar.copy(gate_cols[:], gate_bank[:, 0:8].rearrange("p (r c) -> p r c", r=2))
-        nc.scalar.activation(slope[1, 0][:], a_sb[1, 0][:], ACT.Relu, scale=2.0)
+        nc.scalar.copy(gate_cols[:], gate_bank[:, 0 : 2 * CHUNKS].rearrange("p (r c) -> p r c", r=2))
+        nc.scalar.activation(slope[3][:], a_sb[3][:], ACT.Relu, scale=2.0)
 
+        fetched = {}
         turned = {}
         gated = {}
         da = keep.tile([P, T, 4], BF16, name="da", align_bytes=64)
         da_w = keep.tile([P, T], U32, name="da_w", align_bytes=64)
         da_s = keep.tile([P, T], U8, name="da_s", align_bytes=64)
 
-        def fetch_and_turn(r, t, first, count):
+        def fetch(r, t, first, count):
             lo, hi = P * first, P * (first + count)
-            t_lo = 2 * (t // 2) if first < 2 else 0
+            piece, row, col = slope_of[t, first]
             picked = keep.tile([P, hi - lo], F32, name="picked%d%d%d" % (r, t, first))
             nc.vector.tensor_tensor(
                 picked[:],
-                y[t][:].indirect(pos_sb[r][:, lo // 16 : hi // 16]),
-                slope[first // 2, t_lo][:, t - t_lo, lo % 256 : lo % 256 + hi - lo],
+                y[t][:].indirect(pos_sb[r][:, lo // LIST_COLUMN : hi // LIST_COLUMN]),
+                slope[piece][:, row, col : col + hi - lo],
                 MULT,
             )
-            for c in range(first, first + count):
-                if (r, c) not in turned:
-                    turned[r, c] = psum.tile([P, H], F32, name="turned", tag="bank%d" % TURNED_BANK[r, c])
-                if c < 2:
-                    place = turned[r, c][:, P * t : P * (t + 1)]
+            for chunk in range(first, first + count):
+                fetched[r, t, chunk] = picked[:, P * (chunk - first) : P * (chunk - first + 1)]
+
+        def turn(r, t, first, count):
+            for chunk in range(first, first + count):
+                if (r, chunk) not in turned:
+                    turned[r, chunk] = psum.tile([P, H], F32, name="turned", tag="bank%d" % TURNED_BANK[r, chunk])
+                if chunk < BANK_SUMMED:
+                    place = turned[r, chunk][:, P * t : P * (t + 1)]
                 else:
-                    place = turned[r, c][:].rearrange("n (u p e) -> n p u e", u=2, e=2)[:, 32 * t : 32 * (t + 1)]
-                nc.tensor.transpose(
-                    place, picked[:, P * (c - first) : P * (c - first + 1)], ident[:]
-                )
+                    by_pair = turned[r, chunk][:].rearrange("n (u p v) -> n p u v", u=2, v=2)
+                    place = by_pair[:, P // 4 * t : P // 4 * (t + 1)]
+                nc.tensor.transpose(place, fetched[r, t, chunk], ident[:])
 
-        def gate_first(c):
-            gated[c] = keep.tile([P, H], F32, name="gated%d" % c)
-            nc.scalar.activation(gated[c][:], turned[0, c][:], ACT.Copy, scale=gate_cols[:, 0, c : c + 1])
+        def fetch_and_turn(r, t, first, count):
+            fetch(r, t, first, count)
+            turn(r, t, first, count)
 
-        def sum_and_round(c):
-            rounded = keep.tile([P, H], BF16, name="rounded%d" % c)
-            nc.vector.scalar_tensor_tensor(
-                rounded[:], turned[1, c][:], gate_cols[:, 1, c : c + 1], gated[c][:], MULT, ADD
-            )
-            pairs = rounded[:].bitcast(F32)
-            bank = psum.tile([P, 2, P], F32, name="pair_bank", tag="bank%d" % PAIR_BANK[c])
-            for u in range(2):
-                nc.tensor.transpose(bank[:, u, :], pairs[:, P * u : P * (u + 1)], ident[:])
-            nc.scalar.copy(
-                da[:, P * c : P * (c + 1), :].rearrange("p n j -> p (n j)").bitcast(F32).rearrange("p (n u) -> p n u", u=2),
-                bank[:].rearrange("p u n -> p n u"),
-            )
-
-        def sum_in_bank(c):
-            back = psum.tile([P, 4, P], F32, name="back", tag="bank%d" % PAIR_BANK[c])
+        def sum_in_bank(chunk):
+            summed = psum.tile([P, 4, P], F32, name="summed", tag="bank%d" % RETURN_BANK[chunk])
             for r in range(2):
-                both = keep.tile([P, 4, P], F32, name="both%d%d" % (r, c))
+                by_byte = keep.tile([P, 4, P], F32, name="by_byte%d%d" % (r, chunk))
                 nc.scalar.activation(
-                    both[:], turned[r, c][:].rearrange("n (p d) -> n d p", d=4), ACT.Copy, scale=gate_cols[:, r, c : c + 1]
+                    by_byte[:],
+                    turned[r, chunk][:].rearrange("n (p d) -> n d p", d=4),
+                    ACT.Copy,
+                    scale=gate_cols[:, r, chunk : chunk + 1],
                 )
                 for d in range(4):
                     nc.tensor.matmul(
-                        back[:, d, :],
-                        lhsT=both[:, d, :],
+                        summed[:, d, :],
+                        lhsT=by_byte[:, d, :],
                         rhs=ident[:],
                         is_transpose=True,
                         start=(r == 0 and d == 0),
                         stop=(r == 1 and d == 3),
                     )
-            return back
+            return summed
 
-        def round_out(c, back):
-            nc.scalar.copy(da[:, P * c : P * (c + 1), :], back[:].rearrange("p d n -> p n d"))
+        def round_out(chunk, summed):
+            nc.scalar.copy(da[:, P * chunk : P * (chunk + 1), :], summed[:].rearrange("p d n -> p n d"))
+
+        def gate_first_list(chunk):
+            gated[chunk] = keep.tile([P, H], F32, name="gated%d" % chunk)
+            nc.scalar.activation(
+                gated[chunk][:], turned[0, chunk][:], ACT.Copy, scale=gate_cols[:, 0, chunk : chunk + 1]
+            )
+
+        def sum_on_vector(chunk):
+            rounded = keep.tile([P, H], BF16, name="rounded%d" % chunk)
+            nc.vector.scalar_tensor_tensor(
+                rounded[:], turned[1, chunk][:], gate_cols[:, 1, chunk : chunk + 1], gated[chunk][:], MULT, ADD
+            )
+            pairs = rounded[:].bitcast(F32)
+            pair_bank = psum.tile([P, 2, P], F32, name="pair_bank", tag="bank%d" % RETURN_BANK[chunk])
+            for u in range(2):
+                nc.tensor.transpose(pair_bank[:, u, :], pairs[:, P * u : P * (u + 1)], ident[:])
+            da_pairs = da[:, P * chunk : P * (chunk + 1), :].rearrange("p n d -> p (n d)").bitcast(F32)
+            nc.scalar.copy(da_pairs.rearrange("p (n u) -> p n u", u=2), pair_bank[:].rearrange("p u n -> p n u"))
 
         def quantise(first, count):
             cols = slice(P * first, P * (first + count))
             nc.vector.quantize_mx(
-                out=da_w[:, cols].bitcast(FP8X4), scales=da_s[:, cols], in_=da[:, cols, :].rearrange("p n j -> p (n j)")
+                out=da_w[:, cols].bitcast(FP8X4), scales=da_s[:, cols], in_=da[:, cols, :].rearrange("p n d -> p (n d)")
             )
 
         def project(first, count, h_lo, h_hi):
@@ -225,7 +250,7 @@ def tile_moe_sub_relu2_kernel(
             for h in range(h_lo, h_hi):
                 nc.tensor.matmul_mx(
                     out=bank[:, h - h_lo, :],
-                    lhsT=w1_w[:, 512 * h : 512 * (h + 1)].bitcast(FP8X4),
+                    lhsT=w1_w[:, 4 * P * h : 4 * P * (h + 1)].bitcast(FP8X4),
                     lhsT_scale=w1_s[:, P * h : P * (h + 1)],
                     rhs=da_w[:, cols].bitcast(FP8X4),
                     rhs_scale=da_s[:, cols],
@@ -242,30 +267,36 @@ def tile_moe_sub_relu2_kernel(
                 in_=result[:],
             )
 
-        for t in range(ROW_TILES):
-            if t == 2:
-                nc.vector.tensor_scalar(slope[0, 2][:], a_sb[0, 2][:], 0.0, 2.0, MAX, MULT)
+        for r in range(2):
+            fetch(r, 0, 0, CHUNKS)
+            turn(r, 0, 0, 2)
+        for t in range(1, ROW_TILES):
             for r in range(2):
                 fetch_and_turn(r, t, 0, 2)
-        backs = [sum_in_bank(c) for c in range(2)]
-        for t in range(ROW_TILES):
+        bank_sums = [sum_in_bank(chunk) for chunk in range(BANK_SUMMED)]
+
+        turn(0, 0, 2, 2)
+        for t in range(1, ROW_TILES):
             fetch_and_turn(0, t, 2, 2)
-        round_out(0, backs[0])
-        gate_first(2)
-        round_out(1, backs[1])
-        gate_first(3)
-        for t in range(ROW_TILES):
-            fetch_and_turn(1, t, 2, 1)
+        round_out(0, bank_sums[0])
+        gate_first_list(2)
+        gate_first_list(3)
+        round_out(1, bank_sums[1])
+        turn(1, 0, 2, 2)
+        for t in (1, 2):
+            fetch_and_turn(1, t, 2, 2)
+        for chunk in (2, 3):
+            fetch_and_turn(1, 3, chunk, 1)
+        sum_on_vector(2)
+        sum_on_vector(3)
+
         quantise(0, 2)
-        store(0, 2, 0, 2, project(0, 2, 0, 2), nc.scalar.copy, nc.sync)
-        for t in range(ROW_TILES):
-            fetch_and_turn(1, t, 3, 1)
-        sum_and_round(2)
-        sum_and_round(3)
+        first_bank = project(0, 2, 0, 2)
         quantise(2, 1)
         third_bank = project(2, 1, 0, 2)
         quantise(3, 1)
         last_banks = [project(3, 1, h, h + 1) for h in range(2)]
-        store(2, 1, 0, 2, third_bank, nc.scalar.copy, nc.sync)
+        store(0, 2, 0, 2, first_bank, nc.scalar.copy, nc.sync)
+        store(2, 1, 0, 2, third_bank, nc.vector.tensor_copy, nc.sync)
         store(3, 1, 0, 1, last_banks[0], nc.vector.tensor_copy, nc.sync)
         store(3, 1, 1, 2, last_banks[1], nc.scalar.copy, nc.scalar)

@@ -227,14 +227,18 @@ def tile_moe_sub_relu2_kernel(
             )
 
         def sum_on_vector(chunk):
-            rounded = keep.tile([P, H], BF16, name="rounded%d" % chunk)
-            nc.vector.scalar_tensor_tensor(
-                rounded[:], turned[1, chunk][:], gate_cols[:, 1, chunk : chunk + 1], gated[chunk][:], MULT, ADD
-            )
-            pairs = rounded[:].bitcast(F32)
             pair_bank = psum.tile([P, 2, P], F32, name="pair_bank", tag="bank%d" % RETURN_BANK[chunk])
-            for u in range(2):
-                nc.tensor.transpose(pair_bank[:, u, :], pairs[:, P * u : P * (u + 1)], ident[:])
+            parts = 2 if chunk == CHUNKS - 1 else 1
+            width = H // parts
+            for part in range(parts):
+                cols = slice(width * part, width * (part + 1))
+                rounded = keep.tile([P, width], BF16, name="rounded%d%d" % (chunk, part))
+                nc.vector.scalar_tensor_tensor(
+                    rounded[:], turned[1, chunk][:, cols], gate_cols[:, 1, chunk : chunk + 1], gated[chunk][:, cols], MULT, ADD
+                )
+                pairs = rounded[:].bitcast(F32)
+                for j in range(2 // parts):
+                    nc.tensor.transpose(pair_bank[:, part + j, :], pairs[:, P * j : P * (j + 1)], ident[:])
             da_pairs = da[:, P * chunk : P * (chunk + 1), :].rearrange("p n d -> p (n d)").bitcast(F32)
             nc.scalar.copy(da_pairs.rearrange("p (n u) -> p n u", u=2), pair_bank[:].rearrange("p u n -> p n u"))
 
@@ -270,9 +274,12 @@ def tile_moe_sub_relu2_kernel(
         for r in range(2):
             fetch(r, 0, 0, CHUNKS)
             turn(r, 0, 0, 2)
-        for t in range(1, ROW_TILES):
+        for t in (1, 2):
             for r in range(2):
                 fetch_and_turn(r, t, 0, 2)
+        for chunk in range(BANK_SUMMED):
+            for r in range(2):
+                fetch_and_turn(r, 3, chunk, 1)
         bank_sums = [sum_in_bank(chunk) for chunk in range(BANK_SUMMED)]
 
         turn(0, 0, 2, 2)

@@ -106,8 +106,8 @@ def tile_moe_sub_relu2_kernel(
         nc.sync.dma_start(pos_sb[0][:], pos1)
         nc.sync.dma_start(pos_sb[1][:], pos2)
         load_a(0)
-        load_a(1)
         load_w2(1, 0, E)
+        load_a(1)
         load_a(2)
         nc.gpsimd.dma_start(out=gate_rows[0 : 2 * CHUNKS, :], in_=gate[:, 0, :].rearrange("r (c p) -> r c p", p=P))
         load_a(3)
@@ -145,11 +145,11 @@ def tile_moe_sub_relu2_kernel(
 
         expert_products(0, 0, 3, 0)
         expert_products(0, 3, 7, 1)
-        for piece in range(2):
-            nc.vector.tensor_scalar(slope[piece][:], a_sb[piece][:], 0.0, 2.0, MAX, MULT)
+        nc.vector.tensor_scalar(slope[0][:], a_sb[0][:], 0.0, 2.0, MAX, MULT)
         expert_products(0, 7, 8, 2)
         expert_products(1, 0, 4, 3)
         expert_products(1, 4, 8, 0)
+        nc.scalar.activation(slope[1][:], a_sb[1][:], ACT.Relu, scale=2.0)
         expert_products(2, 0, 4, 4)
         expert_products(2, 4, 8, 5)
         nc.scalar.activation(slope[2][:], a_sb[2][:], ACT.Relu, scale=2.0)

@@ -25,17 +25,16 @@ CHUNKS = T // P
 LIST_COLUMN = 16
 QUADRANT = 32
 PLANES = 4
-BANK_SUMMED = 2
+SPLIT = 3
 
-EXPERT_GROUPS = [(0, 3), (3, 6), (6, 7), (7, 8)]
-
-A_PIECES = [(0, 1, 0, 512), (1, 2, 0, 256), (2, 4, 0, 256), (1, 4, 256, 512)]
-
-ROW_TILE_3_BANKS = (6, 7, 0, 2)
-GATE_BANK = 1
-TURNED_BANK = {(0, 0): 4, (0, 1): 5, (1, 0): 6, (1, 1): 7, (0, 2): 0, (0, 3): 2, (1, 2): 4, (1, 3): 5}
-RETURN_BANK = {0: 3, 1: 1, 2: 7, 3: 3}
-OUT_BANK = {(0, 0): 6, (2, 0): 1, (3, 0): 0, (3, 1): 2}
+WORD_GROUPS = [(0, 3), (3, 6), (6, 7), (7, 8)]
+BYTE_GROUPS = [(0, 3), (3, 6), (6, 8)]
+PRODUCT_GROUPS = [(0, 3, 0), (3, 6, 4), (6, 8, 0)]
+GATE_BANK = 3
+TURNED_BANK = {(1, 0): 4, (1, 1): 5, (1, 2): 6, (0, 0): 7, (0, 1): 0, (0, 2): 1}
+ADDED_BANK = (2, 7)
+RETURN_BANK = {0: 3, 1: 0, 3: 4, 2: 5}
+OUT_BANK = {(0, 0): 2, (3, 0): 7, (2, 0): 3, (2, 1): 0}
 
 
 def tile_moe_sub_relu2_kernel(
@@ -53,18 +52,16 @@ def tile_moe_sub_relu2_kernel(
         w2_s = keep.tile([P, E // PLANES, H], U8, name="w2_s", align_bytes=64)
         w1_s = keep.tile([P, K], U8, name="w1_s", align_bytes=64)
         w1_w = keep.tile([P, 4 * K], U8, name="w1_w", align_bytes=64)
-        w2_w = [keep.tile([P, E, 4 * 2 * P], U8, name="w2_w%d" % half, align_bytes=64) for half in range(2)]
-        a_sb = []
-        slope = []
-        slope_of = {}
-        for piece, (t_lo, t_hi, lo, hi) in enumerate(A_PIECES):
-            a_sb.append(keep.tile([P, t_hi - t_lo, hi - lo], F32, name="a_sb%d" % piece))
-            slope.append(keep.tile([P, t_hi - t_lo, hi - lo], F32, name="slope%d" % piece))
-            for t in range(t_lo, t_hi):
-                for chunk in range(lo // P, hi // P):
-                    slope_of[t, chunk] = (piece, t - t_lo, P * chunk - lo)
+        w2_w = {}
+        w2_tiles = []
+        for e_lo, e_hi, first_bank in PRODUCT_GROUPS:
+            w2_tiles.append(keep.tile([P, e_hi - e_lo, 4 * H], U8, name="w2_w%d" % e_lo, align_bytes=64))
+            for e in range(e_lo, e_hi):
+                w2_w[e] = w2_tiles[-1][:, e - e_lo, :]
+        a_sb = keep.tile([P, 4, T], F32, name="a_sb")
         gate_rows = keep.tile([P, P], F32, name="gate_rows")
         gate_cols = keep.tile([P, 2, CHUNKS], F32, name="gate_cols")
+        gate_wide = keep.tile([P, 2, T - P * SPLIT], F32, name="gate_wide")
         ident = keep.tile([P, P], F32, name="ident")
         y = [keep.tile([P, SLOTS], F32, name="y%d" % t) for t in range(ROW_TILES)]
 
@@ -75,17 +72,10 @@ def tile_moe_sub_relu2_kernel(
                     in_=w2t_scales[PLANES * group : PLANES * (group + 1), 0, 4 * q : 4 * q + 4, :].bitcast(I32),
                 )
 
-        def load_w2(half, e_lo, e_hi):
+        def load_w2(group):
+            e_lo, e_hi, first_bank = PRODUCT_GROUPS[group]
             src = w2t_words[e_lo:e_hi].rearrange("e s p i d -> p (e s) (i d)")
-            width = 4 * 2 * P
-            nc.sync.dma_start(
-                out=w2_w[half][:, e_lo:e_hi, :].bitcast(I32),
-                in_=src[:, :, width * half : width * (half + 1)].bitcast(I32),
-            )
-
-        def load_a(piece):
-            t_lo, t_hi, lo, hi = A_PIECES[piece]
-            nc.sync.dma_start(out=a_sb[piece][:], in_=a[P * t_lo : P * t_hi, lo:hi].rearrange("(t p) n -> p t n", p=P))
+            nc.sync.dma_start(out=w2_tiles[group][:].bitcast(I32), in_=src.bitcast(I32))
 
         nc.vector.memset(w2_s[:].rearrange("p g i -> p (g i)").bitcast(I32), 0)
         nc.vector.memset(w1_s[:].bitcast(I32), 0)
@@ -100,147 +90,134 @@ def tile_moe_sub_relu2_kernel(
                 in_=dy_scales[:, 4 * q : 4 * q + 4, :].broadcast_to([QUADRANT // 4, 4, T]).bitcast(I32),
             )
         nc.scalar.dma_start(out=dy_w[:], in_=dy_words[0].rearrange("p t d -> p (t d)").bitcast(I32))
-        for group in range(E // PLANES):
-            load_w2(0, PLANES * group, PLANES * (group + 1))
-            load_w2_scales(group)
-        nc.sync.dma_start(pos_sb[0][:], pos1)
+        load_w2(0)
+        load_w2_scales(0)
+        load_w2(1)
+        load_w2_scales(1)
+        load_w2(2)
         nc.sync.dma_start(pos_sb[1][:], pos2)
-        load_a(0)
-        load_w2(1, 0, E)
-        load_a(1)
-        load_a(2)
-        nc.gpsimd.dma_start(out=gate_rows[0 : 2 * CHUNKS, :], in_=gate[:, 0, :].rearrange("r (c p) -> r c p", p=P))
-        load_a(3)
+        nc.sync.dma_start(pos_sb[0][:], pos1)
+        nc.sync.dma_start(out=gate_wide[:], in_=gate[:, :, P * SPLIT : T].rearrange("r p n -> p r n"))
+        nc.gpsimd.dma_start(
+            out=gate_rows[0 : 2 * CHUNKS, :], in_=gate[:, 0, :].rearrange("r (c p) -> r c p", p=P)
+        )
+        nc.sync.dma_start(out=a_sb[:], in_=a.rearrange("(p d) n -> p d n", d=4))
         nc.sync.dma_start(out=w1_w[:].bitcast(I32), in_=w1t_words[0].rearrange("p k d -> p (k d)").bitcast(I32))
         for m in range(4):
             nc.sync.dma_start(out=w1_s[m:P:QUADRANT, :].bitcast(I32), in_=w1t_scales[0, m:16:4, :].bitcast(I32))
 
         slot_w, slot_s = {}, {}
-        for e_lo, e_hi in EXPERT_GROUPS:
-            width = C * (e_hi - e_lo)
-            entries = offs_sb[:, e_lo * C // LIST_COLUMN : e_hi * C // LIST_COLUMN]
-            scales = keep.tile([P, width], U8, name="slot_s%d" % e_lo, align_bytes=64)
-            nc.vector.tensor_copy(scales[:], dy_s[:].indirect(entries))
-            words = keep.tile([P, width], U32, name="slot_w%d" % e_lo, align_bytes=64)
-            nc.vector.tensor_copy(words[:], dy_w[:].bitcast(U32).indirect(entries))
-            for e in range(e_lo, e_hi):
-                cols = slice(C * (e - e_lo), C * (e - e_lo + 1))
-                slot_w[e] = words[:, cols]
-                slot_s[e] = scales[:, cols]
 
-        def expert_products(t, e_lo, e_hi, bank_no):
-            bank = psum.tile([P, 4 * C], F32, name="bank", tag="bank%d" % bank_no)
-            for e in range(e_lo, e_hi):
-                weights = w2_w[t // 2][:, e, 4 * P * (t % 2) : 4 * P * (t % 2 + 1)]
-                nc.tensor.matmul_mx(
-                    out=bank[:, C * (e - e_lo) : C * (e - e_lo + 1)],
-                    lhsT=weights.bitcast(FP8X4),
-                    lhsT_scale=w2_s[4 * (e % PLANES) : P, e // PLANES, P * t : P * (t + 1)],
-                    rhs=slot_w[e].bitcast(FP8X4),
-                    rhs_scale=slot_s[e],
-                    start=True,
-                    stop=True,
-                )
-            nc.scalar.copy(y[t][:, C * e_lo : C * e_hi], bank[:, 0 : C * (e_hi - e_lo)])
+        def entries(e_lo, e_hi):
+            return offs_sb[:, e_lo * C // LIST_COLUMN : e_hi * C // LIST_COLUMN]
 
-        expert_products(0, 0, 3, 0)
-        expert_products(0, 3, 7, 1)
-        nc.vector.tensor_scalar(slope[0][:], a_sb[0][:], 0.0, 2.0, MAX, MULT)
-        expert_products(0, 7, 8, 2)
-        expert_products(1, 0, 4, 3)
-        expert_products(1, 4, 8, 0)
-        nc.scalar.activation(slope[1][:], a_sb[1][:], ACT.Relu, scale=2.0)
-        expert_products(2, 0, 4, 4)
-        expert_products(2, 4, 8, 5)
-        nc.scalar.activation(slope[2][:], a_sb[2][:], ACT.Relu, scale=2.0)
-        for pair, bank_no in enumerate(ROW_TILE_3_BANKS):
-            expert_products(3, 2 * pair, 2 * pair + 2, bank_no)
+        byte_end = dict(BYTE_GROUPS)
+        for e_lo, e_hi in WORD_GROUPS:
+            if e_lo in byte_end:
+                scales = keep.tile([P, C * (byte_end[e_lo] - e_lo)], U8, name="slot_s%d" % e_lo, align_bytes=64)
+                nc.vector.tensor_copy(scales[:], dy_s[:].indirect(entries(e_lo, byte_end[e_lo])))
+                for e in range(e_lo, byte_end[e_lo]):
+                    slot_s[e] = scales[:, C * (e - e_lo) : C * (e - e_lo + 1)]
+            words = keep.tile([P, C * (e_hi - e_lo)], U32, name="slot_w%d" % e_lo, align_bytes=64)
+            nc.vector.tensor_copy(words[:], dy_w[:].bitcast(U32).indirect(entries(e_lo, e_hi)))
+            for e in range(e_lo, e_hi):
+                slot_w[e] = words[:, C * (e - e_lo) : C * (e - e_lo + 1)]
+
+        def product(bank, t, e, e_lo):
+            nc.tensor.matmul_mx(
+                out=bank[:, C * (e - e_lo) : C * (e - e_lo + 1)],
+                lhsT=w2_w[e][:, 4 * P * t : 4 * P * (t + 1)].bitcast(FP8X4),
+                lhsT_scale=w2_s[4 * (e % PLANES) : P, e // PLANES, P * t : P * (t + 1)],
+                rhs=slot_w[e].bitcast(FP8X4),
+                rhs_scale=slot_s[e],
+                start=True,
+                stop=True,
+            )
+
+        def products(group, t, engine_copy):
+            e_lo, e_hi, first_bank = PRODUCT_GROUPS[group]
+            bank = psum.tile([P, C * (e_hi - e_lo)], F32, name="bank", tag="bank%d" % (first_bank + t))
+            for e in range(e_lo, e_hi):
+                product(bank, t, e, e_lo)
+            engine_copy(y[t][:, C * e_lo : C * e_hi], bank[:])
+
+        for t in range(ROW_TILES):
+            products(0, t, nc.scalar.copy)
+        products(1, 0, nc.scalar.copy)
+        products(1, 1, nc.vector.tensor_copy)
+        products(2, 0, nc.vector.tensor_copy)
+        products(2, 1, nc.scalar.copy)
+        for t in (2, 3):
+            products(1, t, nc.scalar.copy)
+            products(2, t, nc.scalar.copy)
 
         gate_bank = psum.tile([P, P], F32, name="gate_bank", tag="bank%d" % GATE_BANK)
         nc.tensor.transpose(gate_bank[:], gate_rows[:], ident[:])
-        nc.scalar.copy(gate_cols[:], gate_bank[:, 0 : 2 * CHUNKS].rearrange("p (r c) -> p r c", r=2))
-        nc.scalar.activation(slope[3][:], a_sb[3][:], ACT.Relu, scale=2.0)
+        nc.scalar.activation(
+            gate_cols[:], gate_bank[:, 0 : 2 * CHUNKS].rearrange("p (r c) -> p r c", r=2), ACT.Copy, scale=2.0
+        )
 
         fetched = {}
         turned = {}
-        gated = {}
+        returned = {}
         da = keep.tile([P, T, 4], BF16, name="da", align_bytes=64)
         da_w = keep.tile([P, T], U32, name="da_w", align_bytes=64)
         da_s = keep.tile([P, T], U8, name="da_s", align_bytes=64)
 
         def fetch(r, t, first, count):
             lo, hi = P * first, P * (first + count)
-            piece, row, col = slope_of[t, first]
             picked = keep.tile([P, hi - lo], F32, name="picked%d%d%d" % (r, t, first))
-            nc.vector.tensor_tensor(
-                picked[:],
-                y[t][:].indirect(pos_sb[r][:, lo // LIST_COLUMN : hi // LIST_COLUMN]),
-                slope[piece][:, row, col : col + hi - lo],
-                MULT,
-            )
+            columns = y[t][:].indirect(pos_sb[r][:, lo // LIST_COLUMN : hi // LIST_COLUMN])
+            if first >= SPLIT:
+                nc.vector.tensor_tensor(picked[:], columns, gate_wide[:, r, lo - P * SPLIT : hi - P * SPLIT], MULT)
+            elif r == 0:
+                nc.scalar.activation(picked[:], columns, ACT.Copy)
+            else:
+                nc.vector.tensor_copy(picked[:], columns)
             for chunk in range(first, first + count):
                 fetched[r, t, chunk] = picked[:, P * (chunk - first) : P * (chunk - first + 1)]
 
-        def turn(r, t, first, count):
-            for chunk in range(first, first + count):
-                if (r, chunk) not in turned:
-                    turned[r, chunk] = psum.tile([P, H], F32, name="turned", tag="bank%d" % TURNED_BANK[r, chunk])
-                if chunk < BANK_SUMMED:
-                    place = turned[r, chunk][:, P * t : P * (t + 1)]
-                else:
-                    by_pair = turned[r, chunk][:].rearrange("n (u p v) -> n p u v", u=2, v=2)
-                    place = by_pair[:, P // 4 * t : P // 4 * (t + 1)]
-                nc.tensor.transpose(place, fetched[r, t, chunk], ident[:])
+        def turn(r, t, chunk):
+            if (r, chunk) not in turned:
+                turned[r, chunk] = psum.tile([P, H], F32, name="turned", tag="bank%d" % TURNED_BANK[r, chunk])
+            nc.tensor.transpose(turned[r, chunk][:, P * t : P * (t + 1)], fetched[r, t, chunk], ident[:])
 
-        def fetch_and_turn(r, t, first, count):
-            fetch(r, t, first, count)
-            turn(r, t, first, count)
+        def add_turned(place, r, t, chunk, start, stop):
+            nc.tensor.matmul(place, lhsT=fetched[r, t, chunk], rhs=ident[:], is_transpose=True, start=start, stop=stop)
 
-        def sum_in_bank(chunk):
-            summed = psum.tile([P, 4, P], F32, name="summed", tag="bank%d" % RETURN_BANK[chunk])
-            for r in range(2):
-                by_byte = keep.tile([P, 4, P], F32, name="by_byte%d%d" % (r, chunk))
-                nc.scalar.activation(
-                    by_byte[:],
-                    turned[r, chunk][:].rearrange("n (p d) -> n d p", d=4),
-                    ACT.Copy,
-                    scale=gate_cols[:, r, chunk : chunk + 1],
-                )
+        def bring_back(chunk, parts):
+            returned[chunk] = psum.tile([P, 4, P], F32, name="summed", tag="bank%d" % RETURN_BANK[chunk])
+            for n, by_byte in enumerate(parts):
                 for d in range(4):
                     nc.tensor.matmul(
-                        summed[:, d, :],
+                        returned[chunk][:, d, :],
                         lhsT=by_byte[:, d, :],
                         rhs=ident[:],
                         is_transpose=True,
-                        start=(r == 0 and d == 0),
-                        stop=(r == 1 and d == 3),
+                        start=(n == 0 and d == 0),
+                        stop=(n == len(parts) - 1 and d == 3),
                     )
-            return summed
 
-        def round_out(chunk, summed):
-            nc.scalar.copy(da[:, P * chunk : P * (chunk + 1), :], summed[:].rearrange("p d n -> p n d"))
-
-        def gate_first_list(chunk):
-            gated[chunk] = keep.tile([P, H], F32, name="gated%d" % chunk)
+        def gated(r, chunk):
+            by_byte = keep.tile([P, 4, P], F32, name="by_byte%d%d" % (r, chunk))
             nc.scalar.activation(
-                gated[chunk][:], turned[0, chunk][:], ACT.Copy, scale=gate_cols[:, 0, chunk : chunk + 1]
+                by_byte[:],
+                turned[r, chunk][:].rearrange("n (p d) -> n d p", d=4),
+                ACT.Copy,
+                scale=gate_cols[:, r, chunk : chunk + 1],
             )
+            return by_byte
 
-        def sum_on_vector(chunk):
-            pair_bank = psum.tile([P, 2, P], F32, name="pair_bank", tag="bank%d" % RETURN_BANK[chunk])
-            parts = 2 if chunk == CHUNKS - 1 else 1
-            width = H // parts
-            for part in range(parts):
-                cols = slice(width * part, width * (part + 1))
-                rounded = keep.tile([P, width], BF16, name="rounded%d%d" % (chunk, part))
-                nc.vector.scalar_tensor_tensor(
-                    rounded[:], turned[1, chunk][:, cols], gate_cols[:, 1, chunk : chunk + 1], gated[chunk][:, cols], MULT, ADD
-                )
-                pairs = rounded[:].bitcast(F32)
-                for j in range(2 // parts):
-                    nc.tensor.transpose(pair_bank[:, part + j, :], pairs[:, P * j : P * (j + 1)], ident[:])
-            da_pairs = da[:, P * chunk : P * (chunk + 1), :].rearrange("p n d -> p (n d)").bitcast(F32)
-            nc.scalar.copy(da_pairs.rearrange("p (n u) -> p n u", u=2), pair_bank[:].rearrange("p u n -> p n u"))
+        def finish(chunk):
+            cols = slice(P * chunk, P * (chunk + 1))
+            nc.vector.scalar_tensor_tensor(
+                da[:, cols, :],
+                a_sb[:, :, cols].rearrange("p d n -> p n d"),
+                0.0,
+                returned[chunk][:].rearrange("p d n -> p n d"),
+                MAX,
+                MULT,
+            )
 
         def quantise(first, count):
             cols = slice(P * first, P * (first + count))
@@ -271,39 +248,55 @@ def tile_moe_sub_relu2_kernel(
                 in_=result[:],
             )
 
-        for r in range(2):
-            fetch(r, 0, 0, CHUNKS)
-            turn(r, 0, 0, 2)
-        for t in (1, 2):
-            for r in range(2):
-                fetch_and_turn(r, t, 0, 2)
-        for chunk in range(BANK_SUMMED):
-            for r in range(2):
-                fetch_and_turn(r, 3, chunk, 1)
-        bank_sums = [sum_in_bank(chunk) for chunk in range(BANK_SUMMED)]
+        for t in range(ROW_TILES):
+            for r in (1, 0):
+                fetch(r, t, 0, SPLIT)
+                for chunk in range(SPLIT):
+                    turn(r, t, chunk)
+        sums = keep.tile([P, 4, P], F32, name="sums")
 
-        turn(0, 0, 2, 2)
-        for t in range(1, ROW_TILES):
-            fetch_and_turn(0, t, 2, 2)
-        round_out(0, bank_sums[0])
-        gate_first_list(2)
-        gate_first_list(3)
-        round_out(1, bank_sums[1])
-        turn(1, 0, 2, 2)
-        for t in (1, 2):
-            fetch_and_turn(1, t, 2, 2)
-        for chunk in (2, 3):
-            fetch_and_turn(1, 3, chunk, 1)
-        sum_on_vector(2)
-        sum_on_vector(3)
+        def last_chunk_half(half):
+            added = psum.tile([P, 2 * P], F32, name="added", tag="bank%d" % ADDED_BANK[half])
+            for u in range(2):
+                for r in range(2):
+                    fetch(r, 2 * half + u, 3, 1)
+                    add_turned(added[:, P * u : P * (u + 1)], r, 2 * half + u, 3, (u, r) == (0, 0), (u, r) == (1, 1))
+            return added
 
+        def empty_half(half, added):
+            nc.scalar.activation(
+                sums[:, :, P // 2 * half : P // 2 * (half + 1)],
+                added[:].rearrange("n (p d) -> n d p", d=4),
+                ACT.Copy,
+                scale=2.0,
+            )
+
+        early = last_chunk_half(0)
+        second_of_first = gated(1, 0)
+        first_part = gated(0, 1)
+        bring_back(0, [second_of_first, gated(0, 0)])
+        late = last_chunk_half(1)
+        both = keep.tile([P, 4, P], F32, name="both")
+        nc.vector.scalar_tensor_tensor(
+            both[:], turned[1, 1][:].rearrange("n (p d) -> n d p", d=4), gate_cols[:, 1, 1:2], first_part[:], MULT, ADD
+        )
+        bring_back(1, [both])
+        empty_half(0, early)
+        empty_half(1, late)
+        bring_back(3, [sums])
+        bring_back(2, [gated(1, 2), gated(0, 2)])
+
+        finish(0)
+        finish(1)
+        finish(3)
         quantise(0, 2)
         first_bank = project(0, 2, 0, 2)
-        quantise(2, 1)
-        third_bank = project(2, 1, 0, 2)
+        finish(2)
         quantise(3, 1)
-        last_banks = [project(3, 1, h, h + 1) for h in range(2)]
+        third_bank = project(3, 1, 0, 2)
+        quantise(2, 1)
+        last_banks = [project(2, 1, h, h + 1) for h in range(2)]
         store(0, 2, 0, 2, first_bank, nc.scalar.copy, nc.sync)
-        store(2, 1, 0, 2, third_bank, nc.vector.tensor_copy, nc.sync)
-        store(3, 1, 0, 1, last_banks[0], nc.vector.tensor_copy, nc.sync)
-        store(3, 1, 1, 2, last_banks[1], nc.scalar.copy, nc.scalar)
+        store(3, 1, 0, 2, third_bank, nc.scalar.copy, nc.sync)
+        store(2, 1, 0, 1, last_banks[0], nc.vector.tensor_copy, nc.sync)
+        store(2, 1, 1, 2, last_banks[1], nc.scalar.copy, nc.scalar)

@@ -34,7 +34,7 @@ GATE_BANK = 3
 TURNED_BANK = {(1, 0): 4, (1, 1): 5, (1, 2): 6, (0, 0): 7, (0, 1): 0, (0, 2): 1}
 ADDED_BANK = (2, 7)
 RETURN_BANK = {0: 3, 1: 0, 3: 4, 2: 5}
-OUT_BANK = {(0, 0): 2, (3, 0): 7, (2, 0): 3, (2, 1): 0}
+OUT_BANK = {(0, 0): 2, (1, 0): 1, (3, 0): 7, (2, 0): 3, (2, 1): 0}
 
 
 def tile_moe_sub_relu2_kernel(
@@ -288,15 +288,15 @@ def tile_moe_sub_relu2_kernel(
 
         finish(0)
         finish(1)
+        quantise(0, 1)
+        store(0, 1, 0, 2, project(0, 1, 0, 2), nc.scalar.copy, nc.sync)
         finish(3)
-        quantise(0, 2)
-        first_bank = project(0, 2, 0, 2)
+        quantise(1, 1)
+        store(1, 1, 0, 2, project(1, 1, 0, 2), nc.scalar.copy, nc.sync)
         finish(2)
         quantise(3, 1)
-        third_bank = project(3, 1, 0, 2)
+        store(3, 1, 0, 2, project(3, 1, 0, 2), nc.scalar.copy, nc.sync)
         quantise(2, 1)
         last_banks = [project(2, 1, h, h + 1) for h in range(2)]
-        store(0, 2, 0, 2, first_bank, nc.scalar.copy, nc.sync)
-        store(3, 1, 0, 2, third_bank, nc.scalar.copy, nc.sync)
         store(2, 1, 0, 1, last_banks[0], nc.vector.tensor_copy, nc.sync)
         store(2, 1, 1, 2, last_banks[1], nc.scalar.copy, nc.scalar)

@@ -30,7 +30,7 @@ SPLIT = 3
 WORD_GROUPS = [(0, 3), (3, 6), (6, 7), (7, 8)]
 BYTE_GROUPS = [(0, 3), (3, 6), (6, 8)]
 PRODUCT_GROUPS = [(0, 3, 0), (3, 6, 4), (6, 8, 0)]
-GATE_BANK = 3
+W2_LOADS = [(0, 3, 0, 4), (3, 6, 0, 4), (6, 8, 0, 2), (6, 8, 2, 4)]
 TURNED_BANK = {(1, 0): 4, (1, 1): 5, (1, 2): 6, (0, 0): 7, (0, 1): 0, (0, 2): 1}
 ADDED_BANK = (2, 7)
 RETURN_BANK = {0: 3, 1: 0, 3: 4, 2: 5}
@@ -54,13 +54,14 @@ def tile_moe_sub_relu2_kernel(
         w1_w = keep.tile([P, 4 * K], U8, name="w1_w", align_bytes=64)
         w2_w = {}
         w2_tiles = []
-        for e_lo, e_hi, first_bank in PRODUCT_GROUPS:
-            w2_tiles.append(keep.tile([P, e_hi - e_lo, 4 * H], U8, name="w2_w%d" % e_lo, align_bytes=64))
+        for e_lo, e_hi, t_lo, t_hi in W2_LOADS:
+            piece = keep.tile([P, e_hi - e_lo, 4 * P * (t_hi - t_lo)], U8, name="w2_w%d%d" % (e_lo, t_lo), align_bytes=64)
+            w2_tiles.append(piece)
             for e in range(e_lo, e_hi):
-                w2_w[e] = w2_tiles[-1][:, e - e_lo, :]
+                for t in range(t_lo, t_hi):
+                    w2_w[e, t] = piece[:, e - e_lo, 4 * P * (t - t_lo) : 4 * P * (t - t_lo + 1)]
         a_sb = keep.tile([P, 4, T], F32, name="a_sb")
-        gate_rows = keep.tile([P, P], F32, name="gate_rows")
-        gate_cols = keep.tile([P, 2, CHUNKS], F32, name="gate_cols")
+        gate_cols = [keep.tile([P, SPLIT], F32, name="gate_cols%d" % r) for r in range(2)]
         gate_wide = keep.tile([P, 2, T - P * SPLIT], F32, name="gate_wide")
         ident = keep.tile([P, P], F32, name="ident")
         y = [keep.tile([P, SLOTS], F32, name="y%d" % t) for t in range(ROW_TILES)]
@@ -72,14 +73,13 @@ def tile_moe_sub_relu2_kernel(
                     in_=w2t_scales[PLANES * group : PLANES * (group + 1), 0, 4 * q : 4 * q + 4, :].bitcast(I32),
                 )
 
-        def load_w2(group):
-            e_lo, e_hi, first_bank = PRODUCT_GROUPS[group]
+        def load_w2(piece):
+            e_lo, e_hi, t_lo, t_hi = W2_LOADS[piece]
             src = w2t_words[e_lo:e_hi].rearrange("e s p i d -> p (e s) (i d)")
-            nc.sync.dma_start(out=w2_tiles[group][:].bitcast(I32), in_=src.bitcast(I32))
+            nc.sync.dma_start(out=w2_tiles[piece][:].bitcast(I32), in_=src[:, :, 4 * P * t_lo : 4 * P * t_hi].bitcast(I32))
 
         nc.vector.memset(w2_s[:].rearrange("p g i -> p (g i)").bitcast(I32), 0)
         nc.vector.memset(w1_s[:].bitcast(I32), 0)
-        nc.vector.memset(gate_rows[:], 0.0)
         make_identity(nc, ident[:])
 
         nc.sync.dma_start(offs_sb[:], offs)
@@ -95,12 +95,13 @@ def tile_moe_sub_relu2_kernel(
         load_w2(1)
         load_w2_scales(1)
         load_w2(2)
+        load_w2(3)
         nc.sync.dma_start(pos_sb[1][:], pos2)
         nc.sync.dma_start(pos_sb[0][:], pos1)
         nc.sync.dma_start(out=gate_wide[:], in_=gate[:, :, P * SPLIT : T].rearrange("r p n -> p r n"))
-        nc.gpsimd.dma_start(
-            out=gate_rows[0 : 2 * CHUNKS, :], in_=gate[:, 0, :].rearrange("r (c p) -> r c p", p=P)
-        )
+        with nc.allow_non_contiguous_dma(reason="one gate a partition"):
+            for r in range(2):
+                nc.sync.dma_start(out=gate_cols[r][:], in_=gate[r, 0, 0 : P * SPLIT].rearrange("(c p) -> p c", p=P))
         nc.sync.dma_start(out=a_sb[:], in_=a.rearrange("(p d) n -> p d n", d=4))
         nc.sync.dma_start(out=w1_w[:].bitcast(I32), in_=w1t_words[0].rearrange("p k d -> p (k d)").bitcast(I32))
         for m in range(4):
@@ -126,7 +127,7 @@ def tile_moe_sub_relu2_kernel(
         def product(bank, t, e, e_lo):
             nc.tensor.matmul_mx(
                 out=bank[:, C * (e - e_lo) : C * (e - e_lo + 1)],
-                lhsT=w2_w[e][:, 4 * P * t : 4 * P * (t + 1)].bitcast(FP8X4),
+                lhsT=w2_w[e, t].bitcast(FP8X4),
                 lhsT_scale=w2_s[4 * (e % PLANES) : P, e // PLANES, P * t : P * (t + 1)],
                 rhs=slot_w[e].bitcast(FP8X4),
                 rhs_scale=slot_s[e],
@@ -134,28 +135,22 @@ def tile_moe_sub_relu2_kernel(
                 stop=True,
             )
 
+        def doubled_by_scalar(place, bank, factor):
+            nc.scalar.activation(place, bank, ACT.Copy, scale=factor)
+
         def products(group, t, engine_copy):
             e_lo, e_hi, first_bank = PRODUCT_GROUPS[group]
             bank = psum.tile([P, C * (e_hi - e_lo)], F32, name="bank", tag="bank%d" % (first_bank + t))
             for e in range(e_lo, e_hi):
                 product(bank, t, e, e_lo)
-            engine_copy(y[t][:, C * e_lo : C * e_hi], bank[:])
+            engine_copy(y[t][:, C * e_lo : C * e_hi], bank[:], 2.0)
 
         for t in range(ROW_TILES):
-            products(0, t, nc.scalar.copy)
-        products(1, 0, nc.scalar.copy)
-        products(1, 1, nc.vector.tensor_copy)
-        products(2, 0, nc.vector.tensor_copy)
-        products(2, 1, nc.scalar.copy)
-        for t in (2, 3):
-            products(1, t, nc.scalar.copy)
-            products(2, t, nc.scalar.copy)
-
-        gate_bank = psum.tile([P, P], F32, name="gate_bank", tag="bank%d" % GATE_BANK)
-        nc.tensor.transpose(gate_bank[:], gate_rows[:], ident[:])
-        nc.scalar.activation(
-            gate_cols[:], gate_bank[:, 0 : 2 * CHUNKS].rearrange("p (r c) -> p r c", r=2), ACT.Copy, scale=2.0
-        )
+            products(0, t, doubled_by_scalar)
+        for t in range(ROW_TILES):
+            products(1, t, nc.vector.tensor_scalar_mul if t == 3 else doubled_by_scalar)
+        for t in range(ROW_TILES):
+            products(2, t, nc.vector.tensor_scalar_mul if t == 0 else doubled_by_scalar)
 
         fetched = {}
         turned = {}
@@ -204,7 +199,7 @@ def tile_moe_sub_relu2_kernel(
                 by_byte[:],
                 turned[r, chunk][:].rearrange("n (p d) -> n d p", d=4),
                 ACT.Copy,
-                scale=gate_cols[:, r, chunk : chunk + 1],
+                scale=gate_cols[r][:, chunk : chunk + 1],
             )
             return by_byte
 
@@ -251,7 +246,7 @@ def tile_moe_sub_relu2_kernel(
         for t in range(ROW_TILES):
             for r in (1, 0):
                 fetch(r, t, 0, SPLIT)
-                for chunk in range(SPLIT):
+                for chunk in (1, 0, 2) if r == 0 else range(SPLIT):
                     turn(r, t, chunk)
         sums = keep.tile([P, 4, P], F32, name="sums")
 
@@ -268,7 +263,6 @@ def tile_moe_sub_relu2_kernel(
                 sums[:, :, P // 2 * half : P // 2 * (half + 1)],
                 added[:].rearrange("n (p d) -> n d p", d=4),
                 ACT.Copy,
-                scale=2.0,
             )
 
         early = last_chunk_half(0)
@@ -278,7 +272,7 @@ def tile_moe_sub_relu2_kernel(
         late = last_chunk_half(1)
         both = keep.tile([P, 4, P], F32, name="both")
         nc.vector.scalar_tensor_tensor(
-            both[:], turned[1, 1][:].rearrange("n (p d) -> n d p", d=4), gate_cols[:, 1, 1:2], first_part[:], MULT, ADD
+            both[:], turned[1, 1][:].rearrange("n (p d) -> n d p", d=4), gate_cols[1][:, 1:2], first_part[:], MULT, ADD
         )
         bring_back(1, [both])
         empty_half(0, early)

@@ -68,7 +68,7 @@ def tile_moe_sub_relu2_kernel(
 
         def load_w2_scales(group):
             for q in range(4):
-                nc.sync.dma_start(
+                (nc.scalar if group == 0 and q < 2 else nc.sync).dma_start(
                     out=w2_s[QUADRANT * q : QUADRANT * q + 4 * PLANES, group, :].bitcast(I32),
                     in_=w2t_scales[PLANES * group : PLANES * (group + 1), 0, 4 * q : 4 * q + 4, :].bitcast(I32),
                 )
@@ -148,9 +148,9 @@ def tile_moe_sub_relu2_kernel(
         for t in range(ROW_TILES):
             products(0, t, doubled_by_scalar)
         for t in range(ROW_TILES):
-            products(1, t, nc.vector.tensor_scalar_mul if t == 3 else doubled_by_scalar)
+            products(1, t, nc.vector.tensor_scalar_mul if t == 1 else doubled_by_scalar)
         for t in range(ROW_TILES):
-            products(2, t, nc.vector.tensor_scalar_mul if t == 0 else doubled_by_scalar)
+            products(2, t, nc.vector.tensor_scalar_mul if t < 2 else doubled_by_scalar)
 
         fetched = {}
         turned = {}
@@ -159,13 +159,13 @@ def tile_moe_sub_relu2_kernel(
         da_w = keep.tile([P, T], U32, name="da_w", align_bytes=64)
         da_s = keep.tile([P, T], U8, name="da_s", align_bytes=64)
 
-        def fetch(r, t, first, count):
+        def fetch(r, t, first, count, late=False):
             lo, hi = P * first, P * (first + count)
-            picked = keep.tile([P, hi - lo], F32, name="picked%d%d%d" % (r, t, first))
+            picked = keep.tile([P, hi - lo], F32, name="picked", tag="picked%d%d%d" % ((0, t, 0) if late else (r, t, first)))
             columns = y[t][:].indirect(pos_sb[r][:, lo // LIST_COLUMN : hi // LIST_COLUMN])
             if first >= SPLIT:
                 nc.vector.tensor_tensor(picked[:], columns, gate_wide[:, r, lo - P * SPLIT : hi - P * SPLIT], MULT)
-            elif r == 0:
+            elif r == 0 or late:
                 nc.scalar.activation(picked[:], columns, ACT.Copy)
             else:
                 nc.vector.tensor_copy(picked[:], columns)
@@ -245,8 +245,9 @@ def tile_moe_sub_relu2_kernel(
 
         for t in range(ROW_TILES):
             for r in (1, 0):
-                fetch(r, t, 0, SPLIT)
-                for chunk in (1, 0, 2) if r == 0 else range(SPLIT):
+                count = SPLIT - 1 if (r, t) == (1, ROW_TILES - 1) else SPLIT
+                fetch(r, t, 0, count)
+                for chunk in range(count):
                     turn(r, t, chunk)
         sums = keep.tile([P, 4, P], F32, name="sums")
 
@@ -266,9 +267,8 @@ def tile_moe_sub_relu2_kernel(
             )
 
         early = last_chunk_half(0)
-        second_of_first = gated(1, 0)
+        bring_back(0, [gated(1, 0), gated(0, 0)])
         first_part = gated(0, 1)
-        bring_back(0, [second_of_first, gated(0, 0)])
         late = last_chunk_half(1)
         both = keep.tile([P, 4, P], F32, name="both")
         nc.vector.scalar_tensor_tensor(
@@ -276,9 +276,12 @@ def tile_moe_sub_relu2_kernel(
         )
         bring_back(1, [both])
         empty_half(0, early)
+        fetch(1, ROW_TILES - 1, SPLIT - 1, 1, late=True)
+        turn(1, ROW_TILES - 1, SPLIT - 1)
         empty_half(1, late)
         bring_back(3, [sums])
-        bring_back(2, [gated(1, 2), gated(0, 2)])
+        last_parts = [gated(0, 2), gated(1, 2)]
+        bring_back(2, last_parts)
 
         finish(0)
         finish(1)
@@ -287,9 +290,9 @@ def tile_moe_sub_relu2_kernel(
         finish(3)
         quantise(1, 1)
         store(1, 1, 0, 2, project(1, 1, 0, 2), nc.scalar.copy, nc.sync)
-        finish(2)
         quantise(3, 1)
         store(3, 1, 0, 2, project(3, 1, 0, 2), nc.scalar.copy, nc.sync)
+        finish(2)
         quantise(2, 1)
         last_banks = [project(2, 1, h, h + 1) for h in range(2)]
         store(2, 1, 0, 1, last_banks[0], nc.vector.tensor_copy, nc.sync)

from contextlib import ExitStack

import concourse.mybir as mybir
from concourse.masks import make_identity

K, T, E, C, H, N = 256, 512, 8, 128, 512, 512
FLOPS = 2 * N * H * E * C + 2 * H * K * T

F32 = mybir.dt.float32
BF16 = mybir.dt.bfloat16
I32 = mybir.dt.int32
U32 = mybir.dt.uint32
U16 = mybir.dt.uint16
U8 = mybir.dt.uint8
FP8X4 = mybir.dt.float8_e4m3fn_x4
ACT = mybir.ActivationFunctionType
MULT = mybir.AluOpType.mult
ADD = mybir.AluOpType.add
MAX = mybir.AluOpType.max

P = 128
SLOTS = E * C
ROW_TILES = H // P
CHUNKS = T // P
LIST_COLUMN = 16
QUADRANT = 32
PLANES = 4
SPLIT = 3

WORD_GROUPS = [(0, 3), (3, 6), (6, 7), (7, 8)]
BYTE_GROUPS = [(0, 3), (3, 6), (6, 8)]
PRODUCT_GROUPS = [(0, 3, 0), (3, 6, 4), (6, 8, 0)]
W2_LOADS = [(0, 3, 0, 4), (3, 6, 0, 4), (6, 8, 0, 2), (6, 8, 2, 4)]
TURNED_BANK = {(1, 0): 4, (1, 1): 5, (1, 2): 6, (0, 0): 7, (0, 1): 0, (0, 2): 1}
ADDED_BANK = (2, 7)
RETURN_BANK = {0: 3, 1: 0, 3: 4, 2: 5}
OUT_BANK = {(0, 0): 2, (1, 0): 1, (3, 0): 7, (2, 0): 3, (2, 1): 0}


def tile_moe_sub_relu2_kernel(
    tc, dy_words, dy_scales, w2t_words, w2t_scales, w1t_words, w1t_scales, a, gate, offs, pos1, pos2, out
):
    nc = tc.nc
    with ExitStack() as ctx:
        keep = ctx.enter_context(tc.tile_pool(name="keep", bufs=1))
        psum = ctx.enter_context(tc.psum_pool(name="psum", bufs=1))

        offs_sb = keep.tile([P, SLOTS // LIST_COLUMN], U16, name="offs_sb")
        pos_sb = [keep.tile([P, T // LIST_COLUMN], U16, name="pos_sb%d" % r) for r in range(2)]
        dy_w = keep.tile([P, T], I32, name="dy_w", align_bytes=64)
        dy_s = keep.tile([P, T], U8, name="dy_s", align_bytes=64)
        w2_s = keep.tile([P, E // PLANES, H], U8, name="w2_s", align_bytes=64)
        w1_s = keep.tile([P, K], U8, name="w1_s", align_bytes=64)
        w1_w = keep.tile([P, 4 * K], U8, name="w1_w", align_bytes=64)
        w2_w = {}
        w2_tiles = []
        for e_lo, e_hi, t_lo, t_hi in W2_LOADS:
            piece = keep.tile([P, e_hi - e_lo, 4 * P * (t_hi - t_lo)], U8, name="w2_w%d%d" % (e_lo, t_lo), align_bytes=64)
            w2_tiles.append(piece)
            for e in range(e_lo, e_hi):
                for t in range(t_lo, t_hi):
                    w2_w[e, t] = piece[:, e - e_lo, 4 * P * (t - t_lo) : 4 * P * (t - t_lo + 1)]
        a_sb = keep.tile([P, 4, T], F32, name="a_sb")
        gate_cols = [keep.tile([P, SPLIT], F32, name="gate_cols%d" % r) for r in range(2)]
        gate_wide = keep.tile([P, 2, T - P * SPLIT], F32, name="gate_wide")
        ident = keep.tile([P, P], F32, name="ident")
        y = [keep.tile([P, SLOTS], F32, name="y%d" % t) for t in range(ROW_TILES)]

        def load_w2_scales(group):
            for q in range(4):
                (nc.scalar if group == 0 and q < 2 else nc.sync).dma_start(
                    out=w2_s[QUADRANT * q : QUADRANT * q + 4 * PLANES, group, :].bitcast(I32),
                    in_=w2t_scales[PLANES * group : PLANES * (group + 1), 0, 4 * q : 4 * q + 4, :].bitcast(I32),
                )

        def load_w2(piece):
            e_lo, e_hi, t_lo, t_hi = W2_LOADS[piece]
            src = w2t_words[e_lo:e_hi].rearrange("e s p i d -> p (e s) (i d)")
            nc.sync.dma_start(out=w2_tiles[piece][:].bitcast(I32), in_=src[:, :, 4 * P * t_lo : 4 * P * t_hi].bitcast(I32))

        nc.vector.memset(w2_s[:].rearrange("p g i -> p (g i)").bitcast(I32), 0)
        nc.vector.memset(w1_s[:].bitcast(I32), 0)
        make_identity(nc, ident[:])

        nc.sync.dma_start(offs_sb[:], offs)
        for q in range(4):
            queue = nc.scalar if q < 2 else nc.sync
            queue.dma_start(
                out=dy_s[QUADRANT * q : QUADRANT * (q + 1), :].bitcast(I32),
                in_=dy_scales[:, 4 * q : 4 * q + 4, :].broadcast_to([QUADRANT // 4, 4, T]).bitcast(I32),
            )
        nc.scalar.dma_start(out=dy_w[:], in_=dy_words[0].rearrange("p t d -> p (t d)").bitcast(I32))
        load_w2(0)
        load_w2_scales(0)
        load_w2(1)
        load_w2_scales(1)
        load_w2(2)
        load_w2(3)
        nc.sync.dma_start(pos_sb[1][:], pos2)
        nc.sync.dma_start(pos_sb[0][:], pos1)
        nc.sync.dma_start(out=gate_wide[:], in_=gate[:, :, P * SPLIT : T].rearrange("r p n -> p r n"))
        with nc.allow_non_contiguous_dma(reason="one gate a partition"):
            for r in range(2):
                nc.sync.dma_start(out=gate_cols[r][:], in_=gate[r, 0, 0 : P * SPLIT].rearrange("(c p) -> p c", p=P))
        nc.sync.dma_start(out=a_sb[:], in_=a.rearrange("(p d) n -> p d n", d=4))
        nc.sync.dma_start(out=w1_w[:].bitcast(I32), in_=w1t_words[0].rearrange("p k d -> p (k d)").bitcast(I32))
        for m in range(4):
            nc.sync.dma_start(out=w1_s[m:P:QUADRANT, :].bitcast(I32), in_=w1t_scales[0, m:16:4, :].bitcast(I32))

        slot_w, slot_s = {}, {}

        def entries(e_lo, e_hi):
            return offs_sb[:, e_lo * C // LIST_COLUMN : e_hi * C // LIST_COLUMN]

        byte_end = dict(BYTE_GROUPS)
        for e_lo, e_hi in WORD_GROUPS:
            if e_lo in byte_end:
                scales = keep.tile([P, C * (byte_end[e_lo] - e_lo)], U8, name="slot_s%d" % e_lo, align_bytes=64)
                nc.vector.tensor_copy(scales[:], dy_s[:].indirect(entries(e_lo, byte_end[e_lo])))
                for e in range(e_lo, byte_end[e_lo]):
                    slot_s[e] = scales[:, C * (e - e_lo) : C * (e - e_lo + 1)]
            words = keep.tile([P, C * (e_hi - e_lo)], U32, name="slot_w%d" % e_lo, align_bytes=64)
            nc.vector.tensor_copy(words[:], dy_w[:].bitcast(U32).indirect(entries(e_lo, e_hi)))
            for e in range(e_lo, e_hi):
                slot_w[e] = words[:, C * (e - e_lo) : C * (e - e_lo + 1)]

        def product(bank, t, e, e_lo):
            nc.tensor.matmul_mx(
                out=bank[:, C * (e - e_lo) : C * (e - e_lo + 1)],
                lhsT=w2_w[e, t].bitcast(FP8X4),
                lhsT_scale=w2_s[4 * (e % PLANES) : P, e // PLANES, P * t : P * (t + 1)],
                rhs=slot_w[e].bitcast(FP8X4),
                rhs_scale=slot_s[e],
                start=True,
                stop=True,
            )

        def doubled_by_scalar(place, bank, factor):
            nc.scalar.activation(place, bank, ACT.Copy, scale=factor)

        def products(group, t, engine_copy):
            e_lo, e_hi, first_bank = PRODUCT_GROUPS[group]
            bank = psum.tile([P, C * (e_hi - e_lo)], F32, name="bank", tag="bank%d" % (first_bank + t))
            for e in range(e_lo, e_hi):
                product(bank, t, e, e_lo)
            engine_copy(y[t][:, C * e_lo : C * e_hi], bank[:], 2.0)

        for t in range(ROW_TILES):
            products(0, t, doubled_by_scalar)
        for t in range(ROW_TILES):
            products(1, t, nc.vector.tensor_scalar_mul if t == 1 else doubled_by_scalar)
        for t in range(ROW_TILES):
            products(2, t, nc.vector.tensor_scalar_mul if t < 2 else doubled_by_scalar)

        fetched = {}
        turned = {}
        returned = {}
        da = keep.tile([P, T, 4], BF16, name="da", align_bytes=64)
        da_w = keep.tile([P, T], U32, name="da_w", align_bytes=64)
        da_s = keep.tile([P, T], U8, name="da_s", align_bytes=64)

        def fetch(r, t, first, count, late=False):
            lo, hi = P * first, P * (first + count)
            picked = keep.tile([P, hi - lo], F32, name="picked", tag="picked%d%d%d" % ((0, t, 0) if late else (r, t, first)))
            columns = y[t][:].indirect(pos_sb[r][:, lo // LIST_COLUMN : hi // LIST_COLUMN])
            if first >= SPLIT:
                nc.vector.tensor_tensor(picked[:], columns, gate_wide[:, r, lo - P * SPLIT : hi - P * SPLIT], MULT)
            elif r == 0 or late:
                nc.scalar.activation(picked[:], columns, ACT.Copy)
            else:
                nc.vector.tensor_copy(picked[:], columns)
            for chunk in range(first, first + count):
                fetched[r, t, chunk] = picked[:, P * (chunk - first) : P * (chunk - first + 1)]

        def turn(r, t, chunk):
            if (r, chunk) not in turned:
                turned[r, chunk] = psum.tile([P, H], F32, name="turned", tag="bank%d" % TURNED_BANK[r, chunk])
            nc.tensor.transpose(turned[r, chunk][:, P * t : P * (t + 1)], fetched[r, t, chunk], ident[:])

        def add_turned(place, r, t, chunk, start, stop):
            nc.tensor.matmul(place, lhsT=fetched[r, t, chunk], rhs=ident[:], is_transpose=True, start=start, stop=stop)

        def bring_back(chunk, parts):
            returned[chunk] = psum.tile([P, 4, P], F32, name="summed", tag="bank%d" % RETURN_BANK[chunk])
            for n, by_byte in enumerate(parts):
                for d in range(4):
                    nc.tensor.matmul(
                        returned[chunk][:, d, :],
                        lhsT=by_byte[:, d, :],
                        rhs=ident[:],
                        is_transpose=True,
                        start=(n == 0 and d == 0),
                        stop=(n == len(parts) - 1 and d == 3),
                    )

        def gated(r, chunk):
            by_byte = keep.tile([P, 4, P], F32, name="by_byte%d%d" % (r, chunk))
            nc.scalar.activation(
                by_byte[:],
                turned[r, chunk][:].rearrange("n (p d) -> n d p", d=4),
                ACT.Copy,
                scale=gate_cols[r][:, chunk : chunk + 1],
            )
            return by_byte

        def finish(chunk):
            cols = slice(P * chunk, P * (chunk + 1))
            nc.vector.scalar_tensor_tensor(
                da[:, cols, :],
                a_sb[:, :, cols].rearrange("p d n -> p n d"),
                0.0,
                returned[chunk][:].rearrange("p d n -> p n d"),
                MAX,
                MULT,
            )

        def quantise(first, count):
            cols = slice(P * first, P * (first + count))
            nc.vector.quantize_mx(
                out=da_w[:, cols].bitcast(FP8X4), scales=da_s[:, cols], in_=da[:, cols, :].rearrange("p n d -> p (n d)")
            )

        def project(first, count, h_lo, h_hi):
            cols = slice(P * first, P * (first + count))
            bank = psum.tile([P, h_hi - h_lo, P * count], F32, name="out_bank", tag="bank%d" % OUT_BANK[first, h_lo])
            for h in range(h_lo, h_hi):
                nc.tensor.matmul_mx(
                    out=bank[:, h - h_lo, :],
                    lhsT=w1_w[:, 4 * P * h : 4 * P * (h + 1)].bitcast(FP8X4),
                    lhsT_scale=w1_s[:, P * h : P * (h + 1)],
                    rhs=da_w[:, cols].bitcast(FP8X4),
                    rhs_scale=da_s[:, cols],
                    start=True,
                    stop=True,
                )
            return bank

        def store(first, count, h_lo, h_hi, bank, engine_copy, queue):
            result = keep.tile([P, h_hi - h_lo, P * count], F32, name="result%d%d" % (first, h_lo))
            engine_copy(result[:], bank[:])
            queue.dma_start(
                out=out[P * h_lo : P * h_hi, P * first : P * (first + count)].rearrange("(h p) n -> p h n", p=P),
                in_=result[:],
            )

        for t in range(ROW_TILES):
            for r in (1, 0):
                count = SPLIT - 1 if (r, t) == (1, ROW_TILES - 1) else SPLIT
                fetch(r, t, 0, count)
                for chunk in range(count):
                    turn(r, t, chunk)
        sums = keep.tile([P, 4, P], F32, name="sums")

        def last_chunk_half(half):
            added = psum.tile([P, 2 * P], F32, name="added", tag="bank%d" % ADDED_BANK[half])
            for u in range(2):
                for r in range(2):
                    fetch(r, 2 * half + u, 3, 1)
                    add_turned(added[:, P * u : P * (u + 1)], r, 2 * half + u, 3, (u, r) == (0, 0), (u, r) == (1, 1))
            return added

        def empty_half(half, added):
            nc.scalar.activation(
                sums[:, :, P // 2 * half : P // 2 * (half + 1)],
                added[:].rearrange("n (p d) -> n d p", d=4),
                ACT.Copy,
            )

        early = last_chunk_half(0)
        bring_back(0, [gated(1, 0), gated(0, 0)])
        first_part = gated(0, 1)
        late = last_chunk_half(1)
        both = keep.tile([P, 4, P], F32, name="both")
        nc.vector.scalar_tensor_tensor(
            both[:], turned[1, 1][:].rearrange("n (p d) -> n d p", d=4), gate_cols[1][:, 1:2], first_part[:], MULT, ADD
        )
        bring_back(1, [both])
        empty_half(0, early)
        fetch(1, ROW_TILES - 1, SPLIT - 1, 1, late=True)
        turn(1, ROW_TILES - 1, SPLIT - 1)
        empty_half(1, late)
        bring_back(3, [sums])
        last_parts = [gated(0, 2), gated(1, 2)]
        bring_back(2, last_parts)

        finish(0)
        finish(1)
        quantise(0, 1)
        store(0, 1, 0, 2, project(0, 1, 0, 2), nc.scalar.copy, nc.sync)
        finish(3)
        quantise(1, 1)
        store(1, 1, 0, 2, project(1, 1, 0, 2), nc.scalar.copy, nc.sync)
        quantise(3, 1)
        store(3, 1, 0, 2, project(3, 1, 0, 2), nc.scalar.copy, nc.sync)
        finish(2)
        quantise(2, 1)
        last_banks = [project(2, 1, h, h + 1) for h in range(2)]
        store(2, 1, 0, 1, last_banks[0], nc.vector.tensor_copy, nc.sync)
        store(2, 1, 1, 2, last_banks[1], nc.scalar.copy, nc.scalar)
